import numpy as np
import ml_dtypes


def mxq(x, axis, fmt="e4m3"):
    dtype, down = {"e4m3": (ml_dtypes.float8_e4m3fn, 7), "e5m2": (ml_dtypes.float8_e5m2, 14)}[fmt]
    v = np.moveaxis(np.asarray(x, np.float32).astype(ml_dtypes.bfloat16).astype(np.float64), axis, -1)
    blocks = v.reshape(v.shape[:-1] + (-1, 32))
    amax = np.abs(blocks).max(-1, keepdims=True)
    byte = np.maximum(np.where(amax > 0, np.frexp(amax)[1] - 1 + 127, 0) - down, 1)
    scale = np.exp2(byte - 127.0)
    codes = (blocks / scale).astype(np.float32).astype(dtype).astype(np.float64)
    return np.moveaxis((codes * scale).reshape(v.shape), -1, axis)


WIDE = False


def mx_kscale(k):
    if not WIDE:
        return np.ones(k)
    levels = np.array([10, -10, 5, -5, 0])
    if k % 512:
        return np.exp2(np.random.permutation(np.resize(levels, k // 32))).repeat(32)
    a = np.empty((k // 512, 16))
    for p in range(k // 512):
        a[p, :8] = np.random.permutation(np.resize(levels, 8))
        for g in range(8):
            far = levels[np.abs(levels - a[p, g]) >= 10]
            a[p, g + 8] = far[np.random.randint(len(far))]
    return np.exp2(a.ravel()).repeat(32)


def f64(x):
    return np.asarray(x).astype(np.float64)


def striped(idx):
    return np.tile(idx.reshape(-1, 16).T, (8, 1)).astype(np.uint16)


def unstriped(offs):
    return offs[:16].T.reshape(-1).astype(np.int64)


def pack_weight(w):
    k, n = w.shape
    w = f64(np.asarray(w, np.float32).astype(ml_dtypes.bfloat16)).reshape(k // 32, 32, n)
    amax = np.abs(w).max(1)
    byte = np.clip(np.where(amax > 0, np.frexp(amax)[1] - 1 + 127 - 7, 1), 1, 254)
    scaled = (w * np.exp2(127.0 - byte)[:, None, :]).reshape(k, n).astype(np.float32)
    words = np.ascontiguousarray(scaled.reshape(k // 512, 128, 4, n).transpose(0, 1, 3, 2)).astype(ml_dtypes.float8_e4m3fn).view(np.uint8)
    return words, np.ascontiguousarray(byte.astype(np.uint8).reshape(k // 512, 16, n))


def unpack_weight(words, scales):
    g, p, n, _ = words.shape
    vals = np.ascontiguousarray(words).view(ml_dtypes.float8_e4m3fn).astype(np.float64) * np.repeat(np.exp2(scales.astype(np.float64) - 127.0), 8, axis=1)[..., None]
    return vals.transpose(0, 1, 3, 2).reshape(g * 512, n)


def relu(v):
    return np.maximum(v, 0.0)


def sigmoid(v):
    return 1.0 / (1.0 + np.exp(-np.maximum(v, -700.0)))


K, T, S, N, U = 512, 2048, 1024, 128, 2048


def setup_inputs():
    n = np.random.standard_normal
    s = mx_kscale(K)[:, None]
    packed_xT = pack_weight(n((K, T)) * s)
    return {
        "x_words": packed_xT[0],
        "x_scales": packed_xT[1],
        "mem": n((N, U)).astype(np.float32),
        "w1": (n((K, N)) / np.sqrt(K) / s).astype(np.float32),
        "w2": (n((K, N)) / np.sqrt(K) / s).astype(np.float32),
        "offs": striped(np.random.permutation(T)[:S]),
        "slot": striped(np.random.permutation(U)[:S]),
    }


def reference(x_words, x_scales, mem, w1, w2, offs, slot):
    old = f64(mem)[:, unstriped(slot)]
    xq = unpack_weight(x_words, x_scales)[:, unstriped(offs)]
    g = sigmoid(mxq(f64(w2), 0, "e4m3").T @ xq)
    y = relu(mxq(f64(w1), 0, "e4m3").T @ xq)
    out = f64(mem).copy()
    out[:, unstriped(slot)] = old + g * (y - old)
    return out

@@ -1,0 +1,115 @@
+from contextlib import ExitStack
+
+import concourse.mybir as mybir
+from concourse.masks import make_identity
+
+K, T, S, N, U = 512, 2048, 1024, 128, 2048
+FLOPS = 2 * 2 * K * N * S
+
+F32 = mybir.dt.float32
+BF16 = mybir.dt.bfloat16
+I32 = mybir.dt.int32
+U32 = mybir.dt.uint32
+U16 = mybir.dt.uint16
+U8 = mybir.dt.uint8
+FP8X4 = mybir.dt.float8_e4m3fn_x4
+ACT = mybir.ActivationFunctionType
+MULT = mybir.AluOpType.mult
+
+P = 128
+PACK = 4
+CHUNK = 256
+BLOCKS = CHUNK // P
+CHUNKS = S // CHUNK
+
+
+def tile_picked_gmem_relu_p_kernel(tc, x_words, x_scales, mem, w1, w2, offs, slot, out):
+    nc = tc.nc
+    with ExitStack() as ctx:
+        keep = ctx.enter_context(tc.tile_pool(name="keep", bufs=1))
+        psum = ctx.enter_context(tc.psum_pool(name="psum", bufs=2))
+
+        offs_sb = keep.tile([P, S // 16], U16, name="offs_sb")
+        slot_sb = keep.tile([P, S // 16], U16, name="slot_sb")
+        words = keep.tile([P, T], U32, name="words", align_bytes=64)
+        scales = keep.tile([P, T], U8, name="scales", align_bytes=64)
+        memory = keep.tile([P, U], F32, name="memory", align_bytes=64)
+        w_raw = [keep.tile([P, PACK, N], F32, name="w_raw%d" % i) for i in range(2)]
+        ident = keep.tile([P, P], F32, name="ident")
+        warm = keep.tile([P, 1], F32, name="warm")
+
+        nc.vector.memset(scales[:].bitcast(I32), 0)
+        nc.vector.memset(warm[:], 0.0)
+        nc.scalar.activation(warm[:], warm[:], ACT.Sigmoid)
+        make_identity(nc, ident[:])
+
+        nc.sync.dma_start(offs_sb[:], offs)
+        for raw, w in zip(w_raw, (w1, w2)):
+            nc.sync.dma_start(raw[:], w.rearrange("(p j) n -> p j n", j=PACK))
+        for q in (0, 2, 1, 3):
+            nc.sync.dma_start(scales[32 * q : 32 * q + 4, :].bitcast(I32), x_scales[0, 4 * q : 4 * q + 4, :].bitcast(I32))
+        nc.sync.dma_start(words[:].bitcast(I32), x_words[0].rearrange("p n t -> p (n t)").bitcast(I32))
+        nc.sync.dma_start(slot_sb[:], slot)
+        nc.sync.dma_start(memory[:], mem)
+
+        grouped = keep.tile([P, 2 * N, PACK], BF16, name="grouped", align_bytes=64)
+        for i in range(2):
+            nc.scalar.copy(grouped[:, i * N : (i + 1) * N, :], w_raw[i][:].rearrange("p j n -> p n j"))
+
+        picked_scales = keep.tile([P, S], U8, name="picked_scales", align_bytes=64)
+        nc.vector.tensor_copy(picked_scales[:], scales[:].indirect(offs_sb[:]))
+
+        w_codes = keep.tile([P, 2 * N], U32, name="w_codes", align_bytes=64)
+        w_scales = keep.tile([P, 2 * N], U8, name="w_scales", align_bytes=64)
+        nc.vector.quantize_mx(out=w_codes[:].bitcast(FP8X4), scales=w_scales[:], in_=grouped[:].rearrange("p n j -> p (n j)"))
+
+        def entries(c):
+            return slice(c * CHUNK // 16, (c + 1) * CHUNK // 16)
+
+        y_t, h_t, y_neg, old, e_t = [], [], [], [], []
+        for c in range(CHUNKS):
+            picked = keep.tile([P, CHUNK], U32, name="picked%d" % c, align_bytes=64)
+            nc.vector.tensor_copy(picked[:], words[:].indirect(offs_sb[:, entries(c)]))
+            u_t = psum.tile([P, BLOCKS, 2 * N], F32, name="u_t")
+            for b in range(BLOCKS):
+                nc.tensor.matmul_mx(
+                    out=u_t[:, b, :],
+                    lhsT=picked[:, b * P : (b + 1) * P].bitcast(FP8X4),
+                    lhsT_scale=picked_scales[:, c * CHUNK + b * P : c * CHUNK + (b + 1) * P],
+                    rhs=w_codes[:].bitcast(FP8X4),
+                    rhs_scale=w_scales[:],
+                    start=True,
+                    stop=True,
+                )
+            y_t.append(keep.tile([P, BLOCKS, N], F32, name="y_t%d" % c))
+            h_t.append(keep.tile([P, BLOCKS, N], F32, name="h_t%d" % c))
+            nc.scalar.activation(y_t[c][:], u_t[:, :, 0:N], ACT.Relu)
+            nc.scalar.activation(h_t[c][:], u_t[:, :, N : 2 * N], ACT.Sigmoid, scale=-1.0)
+            y_ps = psum.tile([P, BLOCKS, P], F32, name="y_ps")
+            for b in range(BLOCKS):
+                nc.tensor.transpose(y_ps[:, b, :], y_t[c][:, b, :], ident[:])
+            y_neg.append(keep.tile([P, BLOCKS, P], F32, name="y_neg%d" % c))
+            nc.scalar.activation(y_neg[c][:], y_ps[:], ACT.Copy, scale=-1.0)
+
+        for c in range(CHUNKS):
+            old.append(keep.tile([P, CHUNK], F32, name="old%d" % c))
+            nc.vector.tensor_copy(old[c][:], memory[:].indirect(slot_sb[:, entries(c)]))
+
+        fresh = keep.tile([P, S], F32, name="fresh")
+        for c in range(CHUNKS):
+            d_t = psum.tile([P, BLOCKS, N], F32, name="d_t")
+            for b in range(BLOCKS):
+                nc.tensor.matmul(d_t[:, b, :], lhsT=y_neg[c][:, b, :], rhs=ident[:], start=True, stop=False, is_transpose=True)
+                nc.tensor.matmul(d_t[:, b, :], lhsT=old[c][:, b * P : (b + 1) * P], rhs=ident[:], start=False, stop=True, is_transpose=True)
+            e_t.append(keep.tile([P, BLOCKS, N], F32, name="e_t%d" % c))
+            nc.vector.tensor_tensor(e_t[c][:], d_t[:], h_t[c][:], MULT)
+            new_ps = psum.tile([P, BLOCKS, P], F32, name="new_ps")
+            for b in range(BLOCKS):
+                nc.tensor.matmul(new_ps[:, b, :], lhsT=y_t[c][:, b, :], rhs=ident[:], start=True, stop=False, is_transpose=True)
+                nc.tensor.matmul(new_ps[:, b, :], lhsT=e_t[c][:, b, :], rhs=ident[:], start=False, stop=True, is_transpose=True)
+            nc.scalar.copy(fresh[:, c * CHUNK : (c + 1) * CHUNK], new_ps[:].rearrange("p b n -> p (b n)"))
+
+        for c in range(CHUNKS):
+            nc.vector.tensor_copy(memory[:].indirect(slot_sb[:, entries(c)]), fresh[:, c * CHUNK : (c + 1) * CHUNK])
+
+        nc.sync.dma_start(out, memory[:])

@@ -1,7 +1,6 @@
 from contextlib import ExitStack
 
 import concourse.mybir as mybir
-from concourse.masks import make_identity
 
 K, T, S, N, U = 512, 2048, 1024, 128, 2048
 FLOPS = 2 * 2 * K * N * S
@@ -14,12 +13,11 @@ U16 = mybir.dt.uint16
 U8 = mybir.dt.uint8
 FP8X4 = mybir.dt.float8_e4m3fn_x4
 ACT = mybir.ActivationFunctionType
-MULT = mybir.AluOpType.mult
+ALU = mybir.AluOpType
 
 P = 128
 PACK = 4
 CHUNK = 256
-BLOCKS = CHUNK // P
 CHUNKS = S // CHUNK
 
 
@@ -27,7 +25,7 @@ def tile_picked_gmem_relu_p_kernel(tc, x_words, x_scales, mem, w1, w2, offs, slo
     nc = tc.nc
     with ExitStack() as ctx:
         keep = ctx.enter_context(tc.tile_pool(name="keep", bufs=1))
-        psum = ctx.enter_context(tc.psum_pool(name="psum", bufs=2))
+        psum = ctx.enter_context(tc.psum_pool(name="psum", bufs=1))
 
         offs_sb = keep.tile([P, S // 16], U16, name="offs_sb")
         slot_sb = keep.tile([P, S // 16], U16, name="slot_sb")
@@ -35,19 +33,17 @@ def tile_picked_gmem_relu_p_kernel(tc, x_words, x_scales, mem, w1, w2, offs, slo
         scales = keep.tile([P, T], U8, name="scales", align_bytes=64)
         memory = keep.tile([P, U], F32, name="memory", align_bytes=64)
         w_raw = [keep.tile([P, PACK, N], F32, name="w_raw%d" % i) for i in range(2)]
-        ident = keep.tile([P, P], F32, name="ident")
         warm = keep.tile([P, 1], F32, name="warm")
 
-        nc.vector.memset(scales[:].bitcast(I32), 0)
+        nc.gpsimd.memset(scales[:].bitcast(I32), 0)
         nc.vector.memset(warm[:], 0.0)
         nc.scalar.activation(warm[:], warm[:], ACT.Sigmoid)
-        make_identity(nc, ident[:])
 
         nc.sync.dma_start(offs_sb[:], offs)
-        for raw, w in zip(w_raw, (w1, w2)):
-            nc.sync.dma_start(raw[:], w.rearrange("(p j) n -> p j n", j=PACK))
         for q in (0, 2, 1, 3):
             nc.sync.dma_start(scales[32 * q : 32 * q + 4, :].bitcast(I32), x_scales[0, 4 * q : 4 * q + 4, :].bitcast(I32))
+        for raw, w in zip(w_raw, (w1, w2)):
+            nc.sync.dma_start(raw[:], w.rearrange("(p j) n -> p j n", j=PACK))
         nc.sync.dma_start(words[:].bitcast(I32), x_words[0].rearrange("p n t -> p (n t)").bitcast(I32))
         nc.sync.dma_start(slot_sb[:], slot)
         nc.sync.dma_start(memory[:], mem)
@@ -66,50 +62,38 @@ def tile_picked_gmem_relu_p_kernel(tc, x_words, x_scales, mem, w1, w2, offs, slo
         def entries(c):
             return slice(c * CHUNK // 16, (c + 1) * CHUNK // 16)
 
-        y_t, h_t, y_neg, old, e_t = [], [], [], [], []
+        gate = keep.tile([P, S], F32, name="gate")
+        rest = keep.tile([P, S], F32, name="rest")
+        taken = keep.tile([P, S], F32, name="taken")
+        kept = keep.tile([P, S], F32, name="kept")
+        fresh = keep.tile([P, S], F32, name="fresh")
+        u1 = []
         for c in range(CHUNKS):
+            cols = slice(c * CHUNK, (c + 1) * CHUNK)
             picked = keep.tile([P, CHUNK], U32, name="picked%d" % c, align_bytes=64)
             nc.vector.tensor_copy(picked[:], words[:].indirect(offs_sb[:, entries(c)]))
-            u_t = psum.tile([P, BLOCKS, 2 * N], F32, name="u_t")
-            for b in range(BLOCKS):
+            u1.append(psum.tile([P, CHUNK], F32, name="u1_%d" % c))
+            u2 = psum.tile([P, CHUNK], F32, name="u2_%d" % c)
+            for u, i in ((u2, 1), (u1[c], 0)):
                 nc.tensor.matmul_mx(
-                    out=u_t[:, b, :],
-                    lhsT=picked[:, b * P : (b + 1) * P].bitcast(FP8X4),
-                    lhsT_scale=picked_scales[:, c * CHUNK + b * P : c * CHUNK + (b + 1) * P],
-                    rhs=w_codes[:].bitcast(FP8X4),
-                    rhs_scale=w_scales[:],
+                    out=u[:],
+                    lhsT=w_codes[:, i * N : (i + 1) * N].bitcast(FP8X4),
+                    lhsT_scale=w_scales[:, i * N : (i + 1) * N],
+                    rhs=picked[:].bitcast(FP8X4),
+                    rhs_scale=picked_scales[:, cols],
                     start=True,
                     stop=True,
                 )
-            y_t.append(keep.tile([P, BLOCKS, N], F32, name="y_t%d" % c))
-            h_t.append(keep.tile([P, BLOCKS, N], F32, name="h_t%d" % c))
-            nc.scalar.activation(y_t[c][:], u_t[:, :, 0:N], ACT.Relu)
-            nc.scalar.activation(h_t[c][:], u_t[:, :, N : 2 * N], ACT.Sigmoid, scale=-1.0)
-            y_ps = psum.tile([P, BLOCKS, P], F32, name="y_ps")
-            for b in range(BLOCKS):
-                nc.tensor.transpose(y_ps[:, b, :], y_t[c][:, b, :], ident[:])
-            y_neg.append(keep.tile([P, BLOCKS, P], F32, name="y_neg%d" % c))
-            nc.scalar.activation(y_neg[c][:], y_ps[:], ACT.Copy, scale=-1.0)
+            nc.scalar.activation(gate[:, cols], u2[:], ACT.Sigmoid)
+            nc.scalar.activation(rest[:, cols], u2[:], ACT.Sigmoid, scale=-1.0)
 
         for c in range(CHUNKS):
-            old.append(keep.tile([P, CHUNK], F32, name="old%d" % c))
-            nc.vector.tensor_copy(old[c][:], memory[:].indirect(slot_sb[:, entries(c)]))
-
-        fresh = keep.tile([P, S], F32, name="fresh")
-        for c in range(CHUNKS):
-            d_t = psum.tile([P, BLOCKS, N], F32, name="d_t")
-            for b in range(BLOCKS):
-                nc.tensor.matmul(d_t[:, b, :], lhsT=y_neg[c][:, b, :], rhs=ident[:], start=True, stop=False, is_transpose=True)
-                nc.tensor.matmul(d_t[:, b, :], lhsT=old[c][:, b * P : (b + 1) * P], rhs=ident[:], start=False, stop=True, is_transpose=True)
-            e_t.append(keep.tile([P, BLOCKS, N], F32, name="e_t%d" % c))
-            nc.vector.tensor_tensor(e_t[c][:], d_t[:], h_t[c][:], MULT)
-            new_ps = psum.tile([P, BLOCKS, P], F32, name="new_ps")
-            for b in range(BLOCKS):
-                nc.tensor.matmul(new_ps[:, b, :], lhsT=y_t[c][:, b, :], rhs=ident[:], start=True, stop=False, is_transpose=True)
-                nc.tensor.matmul(new_ps[:, b, :], lhsT=e_t[c][:, b, :], rhs=ident[:], start=False, stop=True, is_transpose=True)
-            nc.scalar.copy(fresh[:, c * CHUNK : (c + 1) * CHUNK], new_ps[:].rearrange("p b n -> p (b n)"))
-
-        for c in range(CHUNKS):
-            nc.vector.tensor_copy(memory[:].indirect(slot_sb[:, entries(c)]), fresh[:, c * CHUNK : (c + 1) * CHUNK])
+            cols = slice(c * CHUNK, (c + 1) * CHUNK)
+            nc.vector.scalar_tensor_tensor(taken[:, cols], u1[c][:], 0.0, gate[:, cols], ALU.max, ALU.mult)
+            nc.vector.tensor_tensor(kept[:, cols], memory[:].indirect(slot_sb[:, entries(c)]), rest[:, cols], ALU.mult)
+        for h in range(2):
+            cols = slice(h * S // 2, (h + 1) * S // 2)
+            nc.vector.tensor_tensor(fresh[:, cols], taken[:, cols], kept[:, cols], ALU.add)
+        nc.vector.tensor_copy(memory[:].indirect(slot_sb[:]), fresh[:])
 
         nc.sync.dma_start(out, memory[:])

@@ -63,11 +63,10 @@ def tile_picked_gmem_relu_p_kernel(tc, x_words, x_scales, mem, w1, w2, offs, slo
             return slice(c * CHUNK // 16, (c + 1) * CHUNK // 16)
 
         gate = keep.tile([P, S], F32, name="gate")
-        rest = keep.tile([P, S], F32, name="rest")
-        taken = keep.tile([P, S], F32, name="taken")
+        cand = keep.tile([P, S], F32, name="cand")
         kept = keep.tile([P, S], F32, name="kept")
         fresh = keep.tile([P, S], F32, name="fresh")
-        u1 = []
+        u1, rest = [], []
         for c in range(CHUNKS):
             cols = slice(c * CHUNK, (c + 1) * CHUNK)
             picked = keep.tile([P, CHUNK], U32, name="picked%d" % c, align_bytes=64)
@@ -84,16 +83,26 @@ def tile_picked_gmem_relu_p_kernel(tc, x_words, x_scales, mem, w1, w2, offs, slo
                     start=True,
                     stop=True,
                 )
-            nc.scalar.activation(gate[:, cols], u2[:], ACT.Sigmoid)
-            nc.scalar.activation(rest[:, cols], u2[:], ACT.Sigmoid, scale=-1.0)
+            rest.append(keep.tile([P, CHUNK], F32, name="rest%d" % c, tag="rest%d" % c))
+            if c == 0:
+                nc.scalar.activation(gate[:, cols], u2[:], ACT.Sigmoid)
+            nc.scalar.activation(rest[c][:], u2[:], ACT.Sigmoid, scale=-1.0)
+            u1[c] = (u1[c], u2)
 
+        taken0 = keep.tile([P, CHUNK], F32, name="taken0")
+        nc.vector.scalar_tensor_tensor(taken0[:], u1[0][0][:], 0.0, gate[:, 0:CHUNK], ALU.max, ALU.mult)
         for c in range(CHUNKS):
             cols = slice(c * CHUNK, (c + 1) * CHUNK)
-            nc.vector.scalar_tensor_tensor(taken[:, cols], u1[c][:], 0.0, gate[:, cols], ALU.max, ALU.mult)
-            nc.vector.tensor_tensor(kept[:, cols], memory[:].indirect(slot_sb[:, entries(c)]), rest[:, cols], ALU.mult)
-        for h in range(2):
-            cols = slice(h * S // 2, (h + 1) * S // 2)
-            nc.vector.tensor_tensor(fresh[:, cols], taken[:, cols], kept[:, cols], ALU.add)
-        nc.vector.tensor_copy(memory[:].indirect(slot_sb[:]), fresh[:])
+            nc.vector.tensor_tensor(kept[:, cols], memory[:].indirect(slot_sb[:, entries(c)]), rest[c][:], ALU.mult)
+        nc.vector.tensor_tensor(fresh[:, 0:CHUNK], taken0[:], kept[:, 0:CHUNK], ALU.add)
+        nc.vector.tensor_copy(memory[:].indirect(slot_sb[:, entries(0)]), fresh[:, 0:CHUNK])
+        for c in range(1, CHUNKS):
+            cols = slice(c * CHUNK, (c + 1) * CHUNK)
+            nc.scalar.activation(gate[:, cols], u1[c][1][:], ACT.Sigmoid)
+            nc.scalar.activation(cand[:, cols], u1[c][0][:], ACT.Relu)
+            taken = keep.tile([P, CHUNK], F32, name="taken%d" % c, tag="rest3")
+            nc.gpsimd.tensor_tensor(taken[:], cand[:, cols], gate[:, cols], ALU.mult)
+            nc.gpsimd.tensor_tensor(fresh[:, cols], taken[:], kept[:, cols], ALU.add)
+            nc.vector.tensor_copy(memory[:].indirect(slot_sb[:, entries(c)]), fresh[:, cols])
 
         nc.sync.dma_start(out, memory[:])

@@ -42,14 +42,14 @@ def tile_picked_gmem_relu_p_kernel(tc, x_words, x_scales, mem, w1, w2, offs, slo
         nc.sync.dma_start(offs_sb[:], offs)
         for q in (0, 2, 1, 3):
             nc.sync.dma_start(scales[32 * q : 32 * q + 4, :].bitcast(I32), x_scales[0, 4 * q : 4 * q + 4, :].bitcast(I32))
-        for raw, w in zip(w_raw, (w1, w2)):
-            nc.sync.dma_start(raw[:], w.rearrange("(p j) n -> p j n", j=PACK))
+        nc.sync.dma_start(w_raw[1][:], w2.rearrange("(p j) n -> p j n", j=PACK))
+        nc.sync.dma_start(w_raw[0][:], w1.rearrange("(p j) n -> p j n", j=PACK))
         nc.sync.dma_start(words[:].bitcast(I32), x_words[0].rearrange("p n t -> p (n t)").bitcast(I32))
         nc.sync.dma_start(slot_sb[:], slot)
         nc.sync.dma_start(memory[:], mem)
 
         grouped = keep.tile([P, 2 * N, PACK], BF16, name="grouped", align_bytes=64)
-        for i in range(2):
+        for i in (1, 0):
             nc.scalar.copy(grouped[:, i * N : (i + 1) * N, :], w_raw[i][:].rearrange("p j n -> p n j"))
 
         picked_scales = keep.tile([P, S], U8, name="picked_scales", align_bytes=64)
@@ -63,7 +63,7 @@ def tile_picked_gmem_relu_p_kernel(tc, x_words, x_scales, mem, w1, w2, offs, slo
             return slice(c * CHUNK // 16, (c + 1) * CHUNK // 16)
 
         gate = keep.tile([P, S], F32, name="gate")
-        cand = keep.tile([P, S], F32, name="cand")
+        cand = keep.tile([P, CHUNK], F32, name="cand")
         kept = keep.tile([P, S], F32, name="kept")
         fresh = keep.tile([P, S], F32, name="fresh")
         u1, rest = [], []
@@ -89,20 +89,36 @@ def tile_picked_gmem_relu_p_kernel(tc, x_words, x_scales, mem, w1, w2, offs, slo
             nc.scalar.activation(rest[c][:], u2[:], ACT.Sigmoid, scale=-1.0)
             u1[c] = (u1[c], u2)
 
-        taken0 = keep.tile([P, CHUNK], F32, name="taken0")
-        nc.vector.scalar_tensor_tensor(taken0[:], u1[0][0][:], 0.0, gate[:, 0:CHUNK], ALU.max, ALU.mult)
-        for c in range(CHUNKS):
-            cols = slice(c * CHUNK, (c + 1) * CHUNK)
-            nc.vector.tensor_tensor(kept[:, cols], memory[:].indirect(slot_sb[:, entries(c)]), rest[c][:], ALU.mult)
-        nc.vector.tensor_tensor(fresh[:, 0:CHUNK], taken0[:], kept[:, 0:CHUNK], ALU.add)
-        nc.vector.tensor_copy(memory[:].indirect(slot_sb[:, entries(0)]), fresh[:, 0:CHUNK])
+        def columns(c):
+            return slice(c * CHUNK, (c + 1) * CHUNK)
+
+        def take(c, tag):
+            taken = keep.tile([P, CHUNK], F32, name="taken%d" % c, tag=tag)
+            nc.vector.scalar_tensor_tensor(taken[:], u1[c][0][:], 0.0, gate[:, columns(c)], ALU.max, ALU.mult)
+            return taken
+
+        def keep_old(c):
+            nc.vector.tensor_tensor(kept[:, columns(c)], memory[:].indirect(slot_sb[:, entries(c)]), rest[c][:], ALU.mult)
+
         for c in range(1, CHUNKS):
-            cols = slice(c * CHUNK, (c + 1) * CHUNK)
-            nc.scalar.activation(gate[:, cols], u1[c][1][:], ACT.Sigmoid)
-            nc.scalar.activation(cand[:, cols], u1[c][0][:], ACT.Relu)
-            taken = keep.tile([P, CHUNK], F32, name="taken%d" % c, tag="rest3")
-            nc.gpsimd.tensor_tensor(taken[:], cand[:, cols], gate[:, cols], ALU.mult)
-            nc.gpsimd.tensor_tensor(fresh[:, cols], taken[:], kept[:, cols], ALU.add)
-            nc.vector.tensor_copy(memory[:].indirect(slot_sb[:, entries(c)]), fresh[:, cols])
+            nc.scalar.activation(gate[:, columns(c)], u1[c][1][:], ACT.Sigmoid)
+        nc.scalar.activation(cand[:], u1[3][0][:], ACT.Relu)
+
+        taken0 = take(0, "taken0")
+        keep_old(0)
+        keep_old(1)
+        nc.vector.tensor_tensor(fresh[:, columns(0)], taken0[:], kept[:, columns(0)], ALU.add)
+        keep_old(2)
+        keep_old(3)
+        taken1 = take(1, "rest2")
+        nc.vector.tensor_copy(memory[:].indirect(slot_sb[:, entries(0)]), fresh[:, columns(0)])
+        nc.gpsimd.tensor_tensor(fresh[:, columns(1)], taken1[:], kept[:, columns(1)], ALU.add)
+        taken2 = take(2, "rest3")
+        nc.vector.tensor_copy(memory[:].indirect(slot_sb[:, entries(1)]), fresh[:, columns(1)])
+        taken3 = keep.tile([P, CHUNK], F32, name="taken3", tag="rest2")
+        nc.gpsimd.tensor_tensor(taken3[:], cand[:], gate[:, columns(3)], ALU.mult)
+        nc.gpsimd.tensor_tensor(fresh[:, columns(3)], taken3[:], kept[:, columns(3)], ALU.add)
+        nc.gpsimd.tensor_tensor(fresh[:, columns(2)], taken2[:], kept[:, columns(2)], ALU.add)
+        nc.vector.tensor_copy(memory[:].indirect(slot_sb[:, 2 * CHUNK // 16 : S // 16]), fresh[:, 2 * CHUNK : S])
 
         nc.sync.dma_start(out, memory[:])

@@ -19,6 +19,8 @@ P = 128
 PACK = 4
 CHUNK = 256
 CHUNKS = S // CHUNK
+HALF = S // 2
+SPLIT = 864
 
 
 def tile_picked_gmem_relu_p_kernel(tc, x_words, x_scales, mem, w1, w2, offs, slot, out):
@@ -48,6 +50,12 @@ def tile_picked_gmem_relu_p_kernel(tc, x_words, x_scales, mem, w1, w2, offs, slo
         nc.sync.dma_start(slot_sb[:], slot)
         nc.sync.dma_start(memory[:], mem)
 
+        def entries(first, last):
+            return slice(first // 16, last // 16)
+
+        def columns(c):
+            return slice(c * CHUNK, (c + 1) * CHUNK)
+
         grouped = keep.tile([P, 2 * N, PACK], BF16, name="grouped", align_bytes=64)
         for i in (1, 0):
             nc.scalar.copy(grouped[:, i * N : (i + 1) * N, :], w_raw[i][:].rearrange("p j n -> p n j"))
@@ -59,66 +67,56 @@ def tile_picked_gmem_relu_p_kernel(tc, x_words, x_scales, mem, w1, w2, offs, slo
         w_scales = keep.tile([P, 2 * N], U8, name="w_scales", align_bytes=64)
         nc.vector.quantize_mx(out=w_codes[:].bitcast(FP8X4), scales=w_scales[:], in_=grouped[:].rearrange("p n j -> p (n j)"))
 
-        def entries(c):
-            return slice(c * CHUNK // 16, (c + 1) * CHUNK // 16)
+        def product(u, i, moving, cols):
+            nc.tensor.matmul_mx(
+                out=u,
+                lhsT=w_codes[:, i * N : (i + 1) * N].bitcast(FP8X4),
+                lhsT_scale=w_scales[:, i * N : (i + 1) * N],
+                rhs=moving.bitcast(FP8X4),
+                rhs_scale=picked_scales[:, cols],
+                start=True,
+                stop=True,
+            )
+
+        u2 = [psum.tile([P, CHUNK], F32, name="u2_%d" % c) for c in range(CHUNKS)]
+        u1_first = psum.tile([P, CHUNK], F32, name="u1_first")
+        u1_middle = psum.tile([P, 2 * CHUNK], F32, name="u1_middle")
+        u1_last = psum.tile([P, CHUNK], F32, name="u1_last")
+        u1 = [u1_first[:], u1_middle[:, columns(0)], u1_middle[:, columns(1)], u1_last[:]]
+        picked = [keep.tile([P, CHUNK], U32, name="picked%d" % c, align_bytes=64) for c in range(CHUNKS)]
+        for c in range(CHUNKS):
+            nc.vector.tensor_copy(picked[c][:], words[:].indirect(offs_sb[:, entries(c * CHUNK, (c + 1) * CHUNK)]))
+            product(u2[c][:], 1, picked[c][:], columns(c))
+            if c == 0:
+                product(u1[c], 0, picked[c][:], columns(c))
+        for c in range(1, CHUNKS):
+            product(u1[c], 0, picked[c][:], columns(c))
 
         gate = keep.tile([P, S], F32, name="gate")
-        cand = keep.tile([P, CHUNK], F32, name="cand")
+        cand = keep.tile([P, S], F32, name="cand")
         kept = keep.tile([P, S], F32, name="kept")
-        fresh = keep.tile([P, S], F32, name="fresh")
-        u1, rest = [], []
+        taken = keep.tile([P, SPLIT + HALF], F32, name="taken")
+        rest_first = keep.tile([P, CHUNK], F32, name="rest_first")
+        rest = [rest_first[:], taken[:, SPLIT - CHUNK : SPLIT], taken[:, SPLIT : SPLIT + CHUNK], taken[:, SPLIT + CHUNK :]]
+
+        def keep_old(first, last, factor):
+            nc.vector.tensor_tensor(kept[:, first:last], memory[:].indirect(slot_sb[:, entries(first, last)]), factor, ALU.mult)
+
+        nc.scalar.activation(gate[:, columns(0)], u2[0][:], ACT.Sigmoid)
+        nc.scalar.activation(cand[:, columns(0)], u1[0], ACT.Relu)
+        nc.gpsimd.tensor_tensor(taken[:, columns(0)], cand[:, columns(0)], gate[:, columns(0)], ALU.mult)
         for c in range(CHUNKS):
-            cols = slice(c * CHUNK, (c + 1) * CHUNK)
-            picked = keep.tile([P, CHUNK], U32, name="picked%d" % c, align_bytes=64)
-            nc.vector.tensor_copy(picked[:], words[:].indirect(offs_sb[:, entries(c)]))
-            u1.append(psum.tile([P, CHUNK], F32, name="u1_%d" % c))
-            u2 = psum.tile([P, CHUNK], F32, name="u2_%d" % c)
-            for u, i in ((u2, 1), (u1[c], 0)):
-                nc.tensor.matmul_mx(
-                    out=u[:],
-                    lhsT=w_codes[:, i * N : (i + 1) * N].bitcast(FP8X4),
-                    lhsT_scale=w_scales[:, i * N : (i + 1) * N],
-                    rhs=picked[:].bitcast(FP8X4),
-                    rhs_scale=picked_scales[:, cols],
-                    start=True,
-                    stop=True,
-                )
-            rest.append(keep.tile([P, CHUNK], F32, name="rest%d" % c, tag="rest%d" % c))
-            if c == 0:
-                nc.scalar.activation(gate[:, cols], u2[:], ACT.Sigmoid)
-            nc.scalar.activation(rest[c][:], u2[:], ACT.Sigmoid, scale=-1.0)
-            u1[c] = (u1[c], u2)
-
-        def columns(c):
-            return slice(c * CHUNK, (c + 1) * CHUNK)
-
-        def take(c, tag):
-            taken = keep.tile([P, CHUNK], F32, name="taken%d" % c, tag=tag)
-            nc.vector.scalar_tensor_tensor(taken[:], u1[c][0][:], 0.0, gate[:, columns(c)], ALU.max, ALU.mult)
-            return taken
-
-        def keep_old(c):
-            nc.vector.tensor_tensor(kept[:, columns(c)], memory[:].indirect(slot_sb[:, entries(c)]), rest[c][:], ALU.mult)
-
+            nc.scalar.activation(rest[c], u2[c][:], ACT.Sigmoid, scale=-1.0)
+        keep_old(0, CHUNK, rest[0])
+        keep_old(CHUNK, HALF, rest[1])
+        keep_old(HALF, S, taken[:, SPLIT:])
         for c in range(1, CHUNKS):
-            nc.scalar.activation(gate[:, columns(c)], u1[c][1][:], ACT.Sigmoid)
-        nc.scalar.activation(cand[:], u1[3][0][:], ACT.Relu)
+            nc.scalar.activation(gate[:, columns(c)], u2[c][:], ACT.Sigmoid)
+        nc.scalar.activation(cand[:, SPLIT:], u1_last[:, SPLIT - 3 * CHUNK :], ACT.Relu)
 
-        taken0 = take(0, "taken0")
-        keep_old(0)
-        keep_old(1)
-        nc.vector.tensor_tensor(fresh[:, columns(0)], taken0[:], kept[:, columns(0)], ALU.add)
-        keep_old(2)
-        keep_old(3)
-        taken1 = take(1, "rest2")
-        nc.vector.tensor_copy(memory[:].indirect(slot_sb[:, entries(0)]), fresh[:, columns(0)])
-        nc.gpsimd.tensor_tensor(fresh[:, columns(1)], taken1[:], kept[:, columns(1)], ALU.add)
-        taken2 = take(2, "rest3")
-        nc.vector.tensor_copy(memory[:].indirect(slot_sb[:, entries(1)]), fresh[:, columns(1)])
-        taken3 = keep.tile([P, CHUNK], F32, name="taken3", tag="rest2")
-        nc.gpsimd.tensor_tensor(taken3[:], cand[:], gate[:, columns(3)], ALU.mult)
-        nc.gpsimd.tensor_tensor(fresh[:, columns(3)], taken3[:], kept[:, columns(3)], ALU.add)
-        nc.gpsimd.tensor_tensor(fresh[:, columns(2)], taken2[:], kept[:, columns(2)], ALU.add)
-        nc.vector.tensor_copy(memory[:].indirect(slot_sb[:, 2 * CHUNK // 16 : S // 16]), fresh[:, 2 * CHUNK : S])
+        nc.vector.scalar_tensor_tensor(taken[:, CHUNK : 3 * CHUNK], u1_middle[:], 0.0, gate[:, CHUNK : 3 * CHUNK], ALU.max, ALU.mult)
+        nc.vector.scalar_tensor_tensor(taken[:, 3 * CHUNK : SPLIT], u1_last[:, : SPLIT - 3 * CHUNK], 0.0, gate[:, 3 * CHUNK : SPLIT], ALU.max, ALU.mult)
+        nc.gpsimd.tensor_tensor(taken[:, SPLIT:S], cand[:, SPLIT:], gate[:, SPLIT:], ALU.mult)
+        nc.vector.tensor_tensor(memory[:].indirect(slot_sb[:]), taken[:, :S], kept[:], ALU.add)
 
         nc.sync.dma_start(out, memory[:])

@@ -20,7 +20,8 @@ PACK = 4
 CHUNK = 256
 CHUNKS = S // CHUNK
 HALF = S // 2
-SPLIT = 864
+SPLIT = 768
+VECTOR_CAST = 64
 
 
 def tile_picked_gmem_relu_p_kernel(tc, x_words, x_scales, mem, w1, w2, offs, slot, out):
@@ -34,19 +35,21 @@ def tile_picked_gmem_relu_p_kernel(tc, x_words, x_scales, mem, w1, w2, offs, slo
         words = keep.tile([P, T], U32, name="words", align_bytes=64)
         scales = keep.tile([P, T], U8, name="scales", align_bytes=64)
         memory = keep.tile([P, U], F32, name="memory", align_bytes=64)
-        w_raw = [keep.tile([P, PACK, N], F32, name="w_raw%d" % i) for i in range(2)]
-        warm = keep.tile([P, 1], F32, name="warm")
+        w2_raw = keep.tile([P, PACK, N], F32, name="w2_raw")
+        w1_raw = keep.tile([P, PACK, N], F32, name="w1_raw")
 
         nc.gpsimd.memset(scales[:].bitcast(I32), 0)
+
+        warm = keep.tile([P, 1], F32, name="warm")
         nc.vector.memset(warm[:], 0.0)
         nc.scalar.activation(warm[:], warm[:], ACT.Sigmoid)
 
+        nc.sync.dma_start(w2_raw[:], w2.rearrange("(p j) n -> p j n", j=PACK))
         nc.sync.dma_start(offs_sb[:], offs)
         for q in (0, 2, 1, 3):
             nc.sync.dma_start(scales[32 * q : 32 * q + 4, :].bitcast(I32), x_scales[0, 4 * q : 4 * q + 4, :].bitcast(I32))
-        nc.sync.dma_start(w_raw[1][:], w2.rearrange("(p j) n -> p j n", j=PACK))
-        nc.sync.dma_start(w_raw[0][:], w1.rearrange("(p j) n -> p j n", j=PACK))
         nc.sync.dma_start(words[:].bitcast(I32), x_words[0].rearrange("p n t -> p (n t)").bitcast(I32))
+        nc.sync.dma_start(w1_raw[:], w1.rearrange("(p j) n -> p j n", j=PACK))
         nc.sync.dma_start(slot_sb[:], slot)
         nc.sync.dma_start(memory[:], mem)
 
@@ -56,67 +59,63 @@ def tile_picked_gmem_relu_p_kernel(tc, x_words, x_scales, mem, w1, w2, offs, slo
         def columns(c):
             return slice(c * CHUNK, (c + 1) * CHUNK)
 
-        grouped = keep.tile([P, 2 * N, PACK], BF16, name="grouped", align_bytes=64)
-        for i in (1, 0):
-            nc.scalar.copy(grouped[:, i * N : (i + 1) * N, :], w_raw[i][:].rearrange("p j n -> p n j"))
+        def quantise(grouped, name):
+            codes = keep.tile([P, N], U32, name=name + "_codes", align_bytes=64)
+            plane = keep.tile([P, N], U8, name=name + "_scales", align_bytes=64)
+            nc.vector.quantize_mx(out=codes[:].bitcast(FP8X4), scales=plane[:], in_=grouped[:].rearrange("p n j -> p (n j)"))
+            return codes, plane
 
-        picked_scales = keep.tile([P, S], U8, name="picked_scales", align_bytes=64)
-        nc.vector.tensor_copy(picked_scales[:], scales[:].indirect(offs_sb[:]))
-
-        w_codes = keep.tile([P, 2 * N], U32, name="w_codes", align_bytes=64)
-        w_scales = keep.tile([P, 2 * N], U8, name="w_scales", align_bytes=64)
-        nc.vector.quantize_mx(out=w_codes[:].bitcast(FP8X4), scales=w_scales[:], in_=grouped[:].rearrange("p n j -> p (n j)"))
-
-        def product(u, i, moving, cols):
+        def product(u, weight, c):
             nc.tensor.matmul_mx(
                 out=u,
-                lhsT=w_codes[:, i * N : (i + 1) * N].bitcast(FP8X4),
-                lhsT_scale=w_scales[:, i * N : (i + 1) * N],
-                rhs=moving.bitcast(FP8X4),
-                rhs_scale=picked_scales[:, cols],
+                lhsT=weight[0][:].bitcast(FP8X4),
+                lhsT_scale=weight[1][:],
+                rhs=picked[c][:].bitcast(FP8X4),
+                rhs_scale=picked_scales[:, columns(c)],
                 start=True,
                 stop=True,
             )
 
+        w2_grouped = keep.tile([P, N, PACK], BF16, name="w2_grouped", align_bytes=64)
+        w1_grouped = keep.tile([P, N, PACK], BF16, name="w1_grouped", align_bytes=64)
+        nc.vector.tensor_copy(w2_grouped[:, :VECTOR_CAST, :], w2_raw[:, :, :VECTOR_CAST].rearrange("p j n -> p n j"))
+        nc.scalar.copy(w2_grouped[:, VECTOR_CAST:, :], w2_raw[:, :, VECTOR_CAST:].rearrange("p j n -> p n j"))
+        w2_mx = quantise(w2_grouped, "w2")
+        nc.scalar.copy(w1_grouped[:], w1_raw[:].rearrange("p j n -> p n j"))
+
+        picked_scales = keep.tile([P, S], U8, name="picked_scales", align_bytes=64)
+        nc.vector.tensor_copy(picked_scales[:], scales[:].indirect(offs_sb[:]))
+
         u2 = [psum.tile([P, CHUNK], F32, name="u2_%d" % c) for c in range(CHUNKS)]
-        u1_first = psum.tile([P, CHUNK], F32, name="u1_first")
-        u1_middle = psum.tile([P, 2 * CHUNK], F32, name="u1_middle")
-        u1_last = psum.tile([P, CHUNK], F32, name="u1_last")
-        u1 = [u1_first[:], u1_middle[:, columns(0)], u1_middle[:, columns(1)], u1_last[:]]
+        u1_front = psum.tile([P, HALF], F32, name="u1_front")
+        u1_back = [psum.tile([P, CHUNK], F32, name="u1_back%d" % c) for c in range(2)]
+        u1 = [u1_front[:, columns(0)], u1_front[:, columns(1)], u1_back[0][:], u1_back[1][:]]
         picked = [keep.tile([P, CHUNK], U32, name="picked%d" % c, align_bytes=64) for c in range(CHUNKS)]
         for c in range(CHUNKS):
             nc.vector.tensor_copy(picked[c][:], words[:].indirect(offs_sb[:, entries(c * CHUNK, (c + 1) * CHUNK)]))
-            product(u2[c][:], 1, picked[c][:], columns(c))
-            if c == 0:
-                product(u1[c], 0, picked[c][:], columns(c))
-        for c in range(1, CHUNKS):
-            product(u1[c], 0, picked[c][:], columns(c))
+            product(u2[c][:], w2_mx, c)
+        w1_mx = quantise(w1_grouped, "w1")
+        for c in (3, 0, 1, 2):
+            product(u1[c], w1_mx, c)
 
         gate = keep.tile([P, S], F32, name="gate")
-        cand = keep.tile([P, S], F32, name="cand")
+        cand = keep.tile([P, S - SPLIT], F32, name="cand")
         kept = keep.tile([P, S], F32, name="kept")
         taken = keep.tile([P, SPLIT + HALF], F32, name="taken")
-        rest_first = keep.tile([P, CHUNK], F32, name="rest_first")
-        rest = [rest_first[:], taken[:, SPLIT - CHUNK : SPLIT], taken[:, SPLIT : SPLIT + CHUNK], taken[:, SPLIT + CHUNK :]]
+        rest = taken[:, SPLIT - HALF :]
 
-        def keep_old(first, last, factor):
-            nc.vector.tensor_tensor(kept[:, first:last], memory[:].indirect(slot_sb[:, entries(first, last)]), factor, ALU.mult)
-
-        nc.scalar.activation(gate[:, columns(0)], u2[0][:], ACT.Sigmoid)
-        nc.scalar.activation(cand[:, columns(0)], u1[0], ACT.Relu)
-        nc.gpsimd.tensor_tensor(taken[:, columns(0)], cand[:, columns(0)], gate[:, columns(0)], ALU.mult)
         for c in range(CHUNKS):
-            nc.scalar.activation(rest[c], u2[c][:], ACT.Sigmoid, scale=-1.0)
-        keep_old(0, CHUNK, rest[0])
-        keep_old(CHUNK, HALF, rest[1])
-        keep_old(HALF, S, taken[:, SPLIT:])
-        for c in range(1, CHUNKS):
+            nc.scalar.activation(rest[:, columns(c)], u2[c][:], ACT.Sigmoid, scale=-1.0)
+        for first in (0, HALF):
+            last = first + HALF
+            nc.vector.tensor_tensor(kept[:, first:last], memory[:].indirect(slot_sb[:, entries(first, last)]), rest[:, first:last], ALU.mult)
+        for c in range(CHUNKS):
             nc.scalar.activation(gate[:, columns(c)], u2[c][:], ACT.Sigmoid)
-        nc.scalar.activation(cand[:, SPLIT:], u1_last[:, SPLIT - 3 * CHUNK :], ACT.Relu)
+        nc.scalar.activation(cand[:], u1_back[1][:, SPLIT - 3 * CHUNK :], ACT.Relu)
 
-        nc.vector.scalar_tensor_tensor(taken[:, CHUNK : 3 * CHUNK], u1_middle[:], 0.0, gate[:, CHUNK : 3 * CHUNK], ALU.max, ALU.mult)
-        nc.vector.scalar_tensor_tensor(taken[:, 3 * CHUNK : SPLIT], u1_last[:, : SPLIT - 3 * CHUNK], 0.0, gate[:, 3 * CHUNK : SPLIT], ALU.max, ALU.mult)
-        nc.gpsimd.tensor_tensor(taken[:, SPLIT:S], cand[:, SPLIT:], gate[:, SPLIT:], ALU.mult)
+        nc.vector.scalar_tensor_tensor(taken[:, :HALF], u1_front[:], 0.0, gate[:, :HALF], ALU.max, ALU.mult)
+        nc.vector.scalar_tensor_tensor(taken[:, columns(2)], u1[2], 0.0, gate[:, columns(2)], ALU.max, ALU.mult)
+        nc.gpsimd.tensor_tensor(taken[:, SPLIT:S], cand[:], gate[:, SPLIT:], ALU.mult)
         nc.vector.tensor_tensor(memory[:].indirect(slot_sb[:]), taken[:, :S], kept[:], ALU.add)
 
         nc.sync.dma_start(out, memory[:])

@@ -20,7 +20,7 @@ PACK = 4
 CHUNK = 256
 CHUNKS = S // CHUNK
 HALF = S // 2
-SPLIT = 768
+SPLIT = 640
 VECTOR_CAST = 64
 
 
@@ -87,35 +87,36 @@ def tile_picked_gmem_relu_p_kernel(tc, x_words, x_scales, mem, w1, w2, offs, slo
         nc.vector.tensor_copy(picked_scales[:], scales[:].indirect(offs_sb[:]))
 
         u2 = [psum.tile([P, CHUNK], F32, name="u2_%d" % c) for c in range(CHUNKS)]
-        u1_front = psum.tile([P, HALF], F32, name="u1_front")
-        u1_back = [psum.tile([P, CHUNK], F32, name="u1_back%d" % c) for c in range(2)]
-        u1 = [u1_front[:, columns(0)], u1_front[:, columns(1)], u1_back[0][:], u1_back[1][:]]
+        u1 = [psum.tile([P, HALF], F32, name="u1_%d" % h) for h in range(2)]
         picked = [keep.tile([P, CHUNK], U32, name="picked%d" % c, align_bytes=64) for c in range(CHUNKS)]
         for c in range(CHUNKS):
             nc.vector.tensor_copy(picked[c][:], words[:].indirect(offs_sb[:, entries(c * CHUNK, (c + 1) * CHUNK)]))
             product(u2[c][:], w2_mx, c)
         w1_mx = quantise(w1_grouped, "w1")
-        for c in (3, 0, 1, 2):
-            product(u1[c], w1_mx, c)
+        for c in (2, 3, 0, 1):
+            product(u1[c // 2][:, columns(c % 2)], w1_mx, c)
 
         gate = keep.tile([P, S], F32, name="gate")
         cand = keep.tile([P, S - SPLIT], F32, name="cand")
         kept = keep.tile([P, S], F32, name="kept")
-        taken = keep.tile([P, SPLIT + HALF], F32, name="taken")
-        rest = taken[:, SPLIT - HALF :]
+        taken = keep.tile([P, S], F32, name="taken")
+        rest_back = keep.tile([P, HALF], F32, name="rest_back")
+        rest = [taken[:, S - HALF - CHUNK // 2 : S - CHUNK // 2], rest_back[:]]
 
         for c in range(CHUNKS):
-            nc.scalar.activation(rest[:, columns(c)], u2[c][:], ACT.Sigmoid, scale=-1.0)
-        for first in (0, HALF):
-            last = first + HALF
-            nc.vector.tensor_tensor(kept[:, first:last], memory[:].indirect(slot_sb[:, entries(first, last)]), rest[:, first:last], ALU.mult)
-        for c in range(CHUNKS):
+            nc.scalar.activation(rest[c // 2][:, columns(c % 2)], u2[c][:], ACT.Sigmoid, scale=-1.0)
+        for h in range(2):
+            first, last = h * HALF, (h + 1) * HALF
+            nc.vector.tensor_tensor(kept[:, first:last], memory[:].indirect(slot_sb[:, entries(first, last)]), rest[h], ALU.mult)
+        for c in (2, 3):
             nc.scalar.activation(gate[:, columns(c)], u2[c][:], ACT.Sigmoid)
-        nc.scalar.activation(cand[:], u1_back[1][:, SPLIT - 3 * CHUNK :], ACT.Relu)
+        nc.scalar.activation(cand[:], u1[1][:, SPLIT - HALF :], ACT.Relu)
+        for c in (0, 1):
+            nc.scalar.activation(gate[:, columns(c)], u2[c][:], ACT.Sigmoid)
 
-        nc.vector.scalar_tensor_tensor(taken[:, :HALF], u1_front[:], 0.0, gate[:, :HALF], ALU.max, ALU.mult)
-        nc.vector.scalar_tensor_tensor(taken[:, columns(2)], u1[2], 0.0, gate[:, columns(2)], ALU.max, ALU.mult)
-        nc.gpsimd.tensor_tensor(taken[:, SPLIT:S], cand[:], gate[:, SPLIT:], ALU.mult)
-        nc.vector.tensor_tensor(memory[:].indirect(slot_sb[:]), taken[:, :S], kept[:], ALU.add)
+        nc.vector.scalar_tensor_tensor(taken[:, :HALF], u1[0][:], 0.0, gate[:, :HALF], ALU.max, ALU.mult)
+        nc.vector.scalar_tensor_tensor(taken[:, HALF:SPLIT], u1[1][:, : SPLIT - HALF], 0.0, gate[:, HALF:SPLIT], ALU.max, ALU.mult)
+        nc.gpsimd.tensor_tensor(taken[:, SPLIT:], cand[:], gate[:, SPLIT:], ALU.mult)
+        nc.vector.tensor_tensor(memory[:].indirect(slot_sb[:]), taken[:], kept[:], ALU.add)
 
         nc.sync.dma_start(out, memory[:])

@@ -20,7 +20,7 @@ PACK = 4
 CHUNK = 256
 CHUNKS = S // CHUNK
 HALF = S // 2
-SPLIT = 640
+SPLIT = 704
 VECTOR_CAST = 64
 
 
@@ -38,7 +38,7 @@ def tile_picked_gmem_relu_p_kernel(tc, x_words, x_scales, mem, w1, w2, offs, slo
         w2_raw = keep.tile([P, PACK, N], F32, name="w2_raw")
         w1_raw = keep.tile([P, PACK, N], F32, name="w1_raw")
 
-        nc.gpsimd.memset(scales[:].bitcast(I32), 0)
+        nc.vector.memset(scales[:].bitcast(I32), 0)
 
         warm = keep.tile([P, 1], F32, name="warm")
         nc.vector.memset(warm[:], 0.0)
@@ -105,14 +105,11 @@ def tile_picked_gmem_relu_p_kernel(tc, x_words, x_scales, mem, w1, w2, offs, slo
 
         for c in range(CHUNKS):
             nc.scalar.activation(rest[c // 2][:, columns(c % 2)], u2[c][:], ACT.Sigmoid, scale=-1.0)
+            nc.scalar.activation(gate[:, columns(c)], u2[c][:], ACT.Sigmoid)
         for h in range(2):
             first, last = h * HALF, (h + 1) * HALF
             nc.vector.tensor_tensor(kept[:, first:last], memory[:].indirect(slot_sb[:, entries(first, last)]), rest[h], ALU.mult)
-        for c in (2, 3):
-            nc.scalar.activation(gate[:, columns(c)], u2[c][:], ACT.Sigmoid)
         nc.scalar.activation(cand[:], u1[1][:, SPLIT - HALF :], ACT.Relu)
-        for c in (0, 1):
-            nc.scalar.activation(gate[:, columns(c)], u2[c][:], ACT.Sigmoid)
 
         nc.vector.scalar_tensor_tensor(taken[:, :HALF], u1[0][:], 0.0, gate[:, :HALF], ALU.max, ALU.mult)
         nc.vector.scalar_tensor_tensor(taken[:, HALF:SPLIT], u1[1][:, : SPLIT - HALF], 0.0, gate[:, HALF:SPLIT], ALU.max, ALU.mult)

@@ -20,7 +20,7 @@ PACK = 4
 CHUNK = 256
 CHUNKS = S // CHUNK
 HALF = S // 2
-SPLIT = 704
+SPLIT = 640
 VECTOR_CAST = 64
 
 

@@ -21,7 +21,6 @@ CHUNK = 256
 CHUNKS = S // CHUNK
 HALF = S // 2
 SPLIT = 640
-VECTOR_CAST = 64
 
 
 def tile_picked_gmem_relu_p_kernel(tc, x_words, x_scales, mem, w1, w2, offs, slot, out):
@@ -78,8 +77,7 @@ def tile_picked_gmem_relu_p_kernel(tc, x_words, x_scales, mem, w1, w2, offs, slo
 
         w2_grouped = keep.tile([P, N, PACK], BF16, name="w2_grouped", align_bytes=64)
         w1_grouped = keep.tile([P, N, PACK], BF16, name="w1_grouped", align_bytes=64)
-        nc.vector.tensor_copy(w2_grouped[:, :VECTOR_CAST, :], w2_raw[:, :, :VECTOR_CAST].rearrange("p j n -> p n j"))
-        nc.scalar.copy(w2_grouped[:, VECTOR_CAST:, :], w2_raw[:, :, VECTOR_CAST:].rearrange("p j n -> p n j"))
+        nc.vector.tensor_copy(w2_grouped[:], w2_raw[:].rearrange("p j n -> p n j"))
         w2_mx = quantise(w2_grouped, "w2")
         nc.scalar.copy(w1_grouped[:], w1_raw[:].rearrange("p j n -> p n j"))
 

@@ -39,18 +39,18 @@ def tile_picked_gmem_relu_p_kernel(tc, x_words, x_scales, mem, w1, w2, offs, slo
 
         nc.vector.memset(scales[:].bitcast(I32), 0)
 
-        warm = keep.tile([P, 1], F32, name="warm")
-        nc.vector.memset(warm[:], 0.0)
-        nc.scalar.activation(warm[:], warm[:], ACT.Sigmoid)
-
-        nc.sync.dma_start(w2_raw[:], w2.rearrange("(p j) n -> p j n", j=PACK))
+        nc.scalar.dma_start(w2_raw[:], w2.rearrange("(p j) n -> p j n", j=PACK))
         nc.sync.dma_start(offs_sb[:], offs)
+        nc.sync.dma_start(slot_sb[:], slot)
         for q in (0, 2, 1, 3):
             nc.sync.dma_start(scales[32 * q : 32 * q + 4, :].bitcast(I32), x_scales[0, 4 * q : 4 * q + 4, :].bitcast(I32))
         nc.sync.dma_start(words[:].bitcast(I32), x_words[0].rearrange("p n t -> p (n t)").bitcast(I32))
         nc.sync.dma_start(w1_raw[:], w1.rearrange("(p j) n -> p j n", j=PACK))
-        nc.sync.dma_start(slot_sb[:], slot)
         nc.sync.dma_start(memory[:], mem)
+
+        warm = keep.tile([P, 1], F32, name="warm")
+        nc.vector.memset(warm[:], 0.0)
+        nc.scalar.activation(warm[:], warm[:], ACT.Sigmoid)
 
         def entries(first, last):
             return slice(first // 16, last // 16)

@@ -77,9 +77,9 @@ def tile_picked_gmem_relu_p_kernel(tc, x_words, x_scales, mem, w1, w2, offs, slo
 
         w2_grouped = keep.tile([P, N, PACK], BF16, name="w2_grouped", align_bytes=64)
         w1_grouped = keep.tile([P, N, PACK], BF16, name="w1_grouped", align_bytes=64)
-        nc.vector.tensor_copy(w2_grouped[:], w2_raw[:].rearrange("p j n -> p n j"))
+        nc.vector.tensor_copy(w2_grouped[:].rearrange("p (c i) j -> p c j i", i=4), w2_raw[:].rearrange("p j (c i) -> p c j i", i=4))
         w2_mx = quantise(w2_grouped, "w2")
-        nc.scalar.copy(w1_grouped[:], w1_raw[:].rearrange("p j n -> p n j"))
+        nc.scalar.copy(w1_grouped[:].rearrange("p (c i) j -> p c j i", i=4), w1_raw[:].rearrange("p j (c i) -> p c j i", i=4))
 
         picked_scales = keep.tile([P, S], U8, name="picked_scales", align_bytes=64)
         nc.vector.tensor_copy(picked_scales[:], scales[:].indirect(offs_sb[:]))

@@ -49,8 +49,7 @@ def tile_picked_gmem_relu_p_kernel(tc, x_words, x_scales, mem, w1, w2, offs, slo
         nc.sync.dma_start(memory[:], mem)
 
         warm = keep.tile([P, 1], F32, name="warm")
-        nc.vector.memset(warm[:], 0.0)
-        nc.scalar.activation(warm[:], warm[:], ACT.Sigmoid)
+        nc.scalar.activation(warm[:], w2_raw[:, 0, 0:1], ACT.Sigmoid)
 
         def entries(first, last):
             return slice(first // 16, last // 16)

@@ -78,7 +78,7 @@ def tile_picked_gmem_relu_p_kernel(tc, x_words, x_scales, mem, w1, w2, offs, slo
         w1_grouped = keep.tile([P, N, PACK], BF16, name="w1_grouped", align_bytes=64)
         nc.vector.tensor_copy(w2_grouped[:].rearrange("p (c i) j -> p c j i", i=4), w2_raw[:].rearrange("p j (c i) -> p c j i", i=4))
         w2_mx = quantise(w2_grouped, "w2")
-        nc.scalar.copy(w1_grouped[:].rearrange("p (c i) j -> p c j i", i=4), w1_raw[:].rearrange("p j (c i) -> p c j i", i=4))
+        nc.gpsimd.tensor_scalar(w1_grouped[:], w1_raw[:].rearrange("p j n -> p n j"), 1.0, 0.0, ALU.mult, ALU.add)
 
         picked_scales = keep.tile([P, S], U8, name="picked_scales", align_bytes=64)
         nc.vector.tensor_copy(picked_scales[:], scales[:].indirect(offs_sb[:]))

@@ -17,10 +17,12 @@ ALU = mybir.AluOpType
 
 P = 128
 PACK = 4
+ROWS = 16
+STACK = P - ROWS
 CHUNK = 256
-CHUNKS = S // CHUNK
-HALF = S // 2
-SPLIT = 640
+EARLY = 640
+HALF = 512
+MEM_FIRST = 512
 
 
 def tile_picked_gmem_relu_p_kernel(tc, x_words, x_scales, mem, w1, w2, offs, slot, out):
@@ -34,28 +36,37 @@ def tile_picked_gmem_relu_p_kernel(tc, x_words, x_scales, mem, w1, w2, offs, slo
         words = keep.tile([P, T], U32, name="words", align_bytes=64)
         scales = keep.tile([P, T], U8, name="scales", align_bytes=64)
         memory = keep.tile([P, U], F32, name="memory", align_bytes=64)
-        w2_raw = keep.tile([P, PACK, N], F32, name="w2_raw")
-        w1_raw = keep.tile([P, PACK, N], F32, name="w1_raw")
-
-        nc.vector.memset(scales[:].bitcast(I32), 0)
-
-        nc.scalar.dma_start(w2_raw[:], w2.rearrange("(p j) n -> p j n", j=PACK))
-        nc.sync.dma_start(offs_sb[:], offs)
-        nc.sync.dma_start(slot_sb[:], slot)
-        for q in (0, 2, 1, 3):
-            nc.sync.dma_start(scales[32 * q : 32 * q + 4, :].bitcast(I32), x_scales[0, 4 * q : 4 * q + 4, :].bitcast(I32))
-        nc.sync.dma_start(words[:].bitcast(I32), x_words[0].rearrange("p n t -> p (n t)").bitcast(I32))
-        nc.sync.dma_start(w1_raw[:], w1.rearrange("(p j) n -> p j n", j=PACK))
-        nc.sync.dma_start(memory[:], mem)
-
-        warm = keep.tile([P, 1], F32, name="warm")
-        nc.scalar.activation(warm[:], w2_raw[:, 0, 0:1], ACT.Sigmoid)
+        w2_raw = keep.tile([P, PACK, N], F32, name="w2_raw", tag="late2", align_bytes=64)
+        w1_raw = keep.tile([P, PACK, N], F32, name="w1_raw", tag="late1", align_bytes=64)
+        stacked = [keep.tile([P, n], U8, name="stacked%d" % h, align_bytes=64) for h, n in enumerate((EARLY, S - EARLY))]
+        planes = [keep.tile([P, n], U8, name="plane%d" % h, align_bytes=64) for h, n in enumerate((EARLY, S - EARLY))]
 
         def entries(first, last):
             return slice(first // 16, last // 16)
 
-        def columns(c):
-            return slice(c * CHUNK, (c + 1) * CHUNK)
+        nc.vector.memset(scales[:STACK, :].bitcast(I32), 0)
+        for plane in planes:
+            nc.vector.memset(plane[:].bitcast(I32), 0)
+
+        nc.sync.dma_start(scales[STACK:, :].bitcast(I32), x_scales[0].bitcast(I32))
+        nc.sync.dma_start(offs_sb[:], offs)
+        nc.sync.dma_start(words[:].bitcast(I32), x_words[0].rearrange("p n t -> p (n t)").bitcast(I32))
+        nc.sync.dma_start(slot_sb[:], slot)
+        nc.sync.dma_start(w2_raw[:], w2.rearrange("(p j) n -> p j n", j=PACK))
+        nc.sync.dma_start(w1_raw[:], w1.rearrange("(p j) n -> p j n", j=PACK))
+        nc.sync.dma_start(memory[:, :MEM_FIRST], mem[:, :MEM_FIRST])
+
+        def pick_scales(part, first, last):
+            nc.vector.tensor_copy(stacked[part][:], scales[:].indirect(offs_sb[:, entries(first, last)]))
+            for q in (0, 2, 1, 3):
+                nc.sync.dma_start(
+                    planes[part][32 * q : 32 * q + 4, :].bitcast(I32),
+                    stacked[part][STACK + 4 * q : STACK + 4 * q + 4, :].bitcast(I32),
+                )
+
+        pick_scales(0, 0, EARLY)
+        nc.sync.dma_start(memory[:, MEM_FIRST:], mem[:, MEM_FIRST:])
+        pick_scales(1, EARLY, S)
 
         def quantise(grouped, name):
             codes = keep.tile([P, N], U32, name=name + "_codes", align_bytes=64)
@@ -63,54 +74,73 @@ def tile_picked_gmem_relu_p_kernel(tc, x_words, x_scales, mem, w1, w2, offs, slo
             nc.vector.quantize_mx(out=codes[:].bitcast(FP8X4), scales=plane[:], in_=grouped[:].rearrange("p n j -> p (n j)"))
             return codes, plane
 
-        def product(u, weight, c):
+        def product(bank, base, weight, first, last):
+            tile, start = [(t, a) for t, a in picked if a <= first][-1]
+            part, origin = (0, 0) if first < EARLY else (1, EARLY)
             nc.tensor.matmul_mx(
-                out=u,
+                out=bank[:, first - base : last - base],
                 lhsT=weight[0][:].bitcast(FP8X4),
                 lhsT_scale=weight[1][:],
-                rhs=picked[c][:].bitcast(FP8X4),
-                rhs_scale=picked_scales[:, columns(c)],
+                rhs=tile[:, first - start : last - start].bitcast(FP8X4),
+                rhs_scale=planes[part][:, first - origin : last - origin],
                 start=True,
                 stop=True,
             )
 
         w2_grouped = keep.tile([P, N, PACK], BF16, name="w2_grouped", align_bytes=64)
         w1_grouped = keep.tile([P, N, PACK], BF16, name="w1_grouped", align_bytes=64)
-        nc.vector.tensor_copy(w2_grouped[:].rearrange("p (c i) j -> p c j i", i=4), w2_raw[:].rearrange("p j (c i) -> p c j i", i=4))
-        w2_mx = quantise(w2_grouped, "w2")
+        nc.gpsimd.tensor_scalar(w2_grouped[:], w2_raw[:].rearrange("p j n -> p n j"), 1.0, 0.0, ALU.mult, ALU.add)
         nc.gpsimd.tensor_scalar(w1_grouped[:], w1_raw[:].rearrange("p j n -> p n j"), 1.0, 0.0, ALU.mult, ALU.add)
 
-        picked_scales = keep.tile([P, S], U8, name="picked_scales", align_bytes=64)
-        nc.vector.tensor_copy(picked_scales[:], scales[:].indirect(offs_sb[:]))
-
-        u2 = [psum.tile([P, CHUNK], F32, name="u2_%d" % c) for c in range(CHUNKS)]
-        u1 = [psum.tile([P, HALF], F32, name="u1_%d" % h) for h in range(2)]
-        picked = [keep.tile([P, CHUNK], U32, name="picked%d" % c, align_bytes=64) for c in range(CHUNKS)]
-        for c in range(CHUNKS):
-            nc.vector.tensor_copy(picked[c][:], words[:].indirect(offs_sb[:, entries(c * CHUNK, (c + 1) * CHUNK)]))
-            product(u2[c][:], w2_mx, c)
+        picked01 = keep.tile([P, HALF], U32, name="picked01", align_bytes=64)
+        nc.vector.tensor_copy(picked01[:], words[:].indirect(offs_sb[:, entries(0, HALF)]))
+        w2_mx = quantise(w2_grouped, "w2")
+        picked2 = keep.tile([P, CHUNK], U32, name="picked2", tag="late2", align_bytes=64)
+        nc.vector.tensor_copy(picked2[:], words[:].indirect(offs_sb[:, entries(2 * CHUNK, 3 * CHUNK)]))
         w1_mx = quantise(w1_grouped, "w1")
-        for c in (2, 3, 0, 1):
-            product(u1[c // 2][:, columns(c % 2)], w1_mx, c)
+        picked3 = keep.tile([P, CHUNK], U32, name="picked3", tag="late1", align_bytes=64)
+        nc.vector.tensor_copy(picked3[:], words[:].indirect(offs_sb[:, entries(3 * CHUNK, S)]))
+        picked = [(picked01, 0), (picked2, 2 * CHUNK), (picked3, 3 * CHUNK)]
+
+        gate_parts = [(0, CHUNK), (CHUNK, EARLY), (EARLY, S)]
+        cand_parts = [(0, CHUNK), (CHUNK, HALF), (HALF, S)]
+        u2 = [psum.tile([P, b - a], F32, name="u2_%d" % a) for a, b in gate_parts]
+        u1 = [psum.tile([P, b - a], F32, name="u1_%d" % a) for a, b in cand_parts]
+        product(u2[0], 0, w2_mx, 0, CHUNK)
+        product(u2[1], CHUNK, w2_mx, CHUNK, HALF)
+        product(u2[1], CHUNK, w2_mx, HALF, EARLY)
+        product(u1[0], 0, w1_mx, 0, CHUNK)
+        product(u1[1], CHUNK, w1_mx, CHUNK, HALF)
+        product(u1[2], HALF, w1_mx, HALF, EARLY)
+        for bank, base, weight in ((u2[2], EARLY, w2_mx), (u1[2], HALF, w1_mx)):
+            product(bank, base, weight, EARLY, 3 * CHUNK)
+            product(bank, base, weight, 3 * CHUNK, S)
 
         gate = keep.tile([P, S], F32, name="gate")
-        cand = keep.tile([P, S - SPLIT], F32, name="cand")
+        cand = keep.tile([P, CHUNK], F32, name="cand")
         kept = keep.tile([P, S], F32, name="kept")
         taken = keep.tile([P, S], F32, name="taken")
-        rest_back = keep.tile([P, HALF], F32, name="rest_back")
-        rest = [taken[:, S - HALF - CHUNK // 2 : S - CHUNK // 2], rest_back[:]]
+        rest_first = keep.tile([P, CHUNK], F32, name="rest_first")
+        rest_last = keep.tile([P, S - EARLY], F32, name="rest_last")
+        rest = [rest_first[:], taken[:, CHUNK:EARLY], rest_last[:]]
 
-        for c in range(CHUNKS):
-            nc.scalar.activation(rest[c // 2][:, columns(c % 2)], u2[c][:], ACT.Sigmoid, scale=-1.0)
-            nc.scalar.activation(gate[:, columns(c)], u2[c][:], ACT.Sigmoid)
-        for h in range(2):
-            first, last = h * HALF, (h + 1) * HALF
-            nc.vector.tensor_tensor(kept[:, first:last], memory[:].indirect(slot_sb[:, entries(first, last)]), rest[h], ALU.mult)
-        nc.scalar.activation(cand[:], u1[1][:, SPLIT - HALF :], ACT.Relu)
+        def factor(dst, part, sign):
+            nc.scalar.activation(dst, u2[part][:], ACT.Sigmoid, scale=sign)
 
-        nc.vector.scalar_tensor_tensor(taken[:, :HALF], u1[0][:], 0.0, gate[:, :HALF], ALU.max, ALU.mult)
-        nc.vector.scalar_tensor_tensor(taken[:, HALF:SPLIT], u1[1][:, : SPLIT - HALF], 0.0, gate[:, HALF:SPLIT], ALU.max, ALU.mult)
-        nc.gpsimd.tensor_tensor(taken[:, SPLIT:], cand[:], gate[:, SPLIT:], ALU.mult)
+        factor(gate[:, :CHUNK], 0, 1.0)
+        factor(rest[0], 0, -1.0)
+        factor(rest[1], 1, -1.0)
+        factor(gate[:, CHUNK:EARLY], 1, 1.0)
+        factor(rest[2], 2, -1.0)
+        nc.scalar.activation(cand[:], u1[1][:], ACT.Relu)
+        factor(gate[:, EARLY:], 2, 1.0)
+
+        nc.vector.scalar_tensor_tensor(taken[:, :CHUNK], u1[0][:], 0.0, gate[:, :CHUNK], ALU.max, ALU.mult)
+        for part, (first, last) in enumerate(gate_parts):
+            nc.vector.tensor_tensor(kept[:, first:last], memory[:].indirect(slot_sb[:, entries(first, last)]), rest[part], ALU.mult)
+
+        nc.gpsimd.tensor_tensor(taken[:, CHUNK:HALF], cand[:], gate[:, CHUNK:HALF], ALU.mult)
+        nc.vector.scalar_tensor_tensor(taken[:, HALF:], u1[2][:], 0.0, gate[:, HALF:], ALU.max, ALU.mult)
         nc.vector.tensor_tensor(memory[:].indirect(slot_sb[:]), taken[:], kept[:], ALU.add)
 
         nc.sync.dma_start(out, memory[:])

@@ -56,6 +56,9 @@ def tile_picked_gmem_relu_p_kernel(tc, x_words, x_scales, mem, w1, w2, offs, slo
         nc.sync.dma_start(w1_raw[:], w1.rearrange("(p j) n -> p j n", j=PACK))
         nc.sync.dma_start(memory[:, :MEM_FIRST], mem[:, :MEM_FIRST])
 
+        warm = keep.tile([P, 1], F32, name="warm")
+        nc.scalar.activation(warm[:], w2_raw[:, 0, 0:1], ACT.Sigmoid)
+
         def pick_scales(part, first, last):
             nc.vector.tensor_copy(stacked[part][:], scales[:].indirect(offs_sb[:, entries(first, last)]))
             for q in (0, 2, 1, 3):
@@ -89,8 +92,8 @@ def tile_picked_gmem_relu_p_kernel(tc, x_words, x_scales, mem, w1, w2, offs, slo
 
         w2_grouped = keep.tile([P, N, PACK], BF16, name="w2_grouped", align_bytes=64)
         w1_grouped = keep.tile([P, N, PACK], BF16, name="w1_grouped", align_bytes=64)
-        nc.gpsimd.tensor_scalar(w2_grouped[:], w2_raw[:].rearrange("p j n -> p n j"), 1.0, 0.0, ALU.mult, ALU.add)
-        nc.gpsimd.tensor_scalar(w1_grouped[:], w1_raw[:].rearrange("p j n -> p n j"), 1.0, 0.0, ALU.mult, ALU.add)
+        for grouped, raw in ((w2_grouped, w2_raw), (w1_grouped, w1_raw)):
+            nc.scalar.copy(grouped[:].rearrange("p (c i) j -> p c j i", i=4), raw[:].rearrange("p j (c i) -> p c j i", i=4))
 
         picked01 = keep.tile([P, HALF], U32, name="picked01", align_bytes=64)
         nc.vector.tensor_copy(picked01[:], words[:].indirect(offs_sb[:, entries(0, HALF)]))

@@ -22,7 +22,7 @@ STACK = P - ROWS
 CHUNK = 256
 EARLY = 640
 HALF = 512
-MEM_FIRST = 512
+MEM_FIRST = 736
 
 
 def tile_picked_gmem_relu_p_kernel(tc, x_words, x_scales, mem, w1, w2, offs, slot, out):
@@ -36,8 +36,8 @@ def tile_picked_gmem_relu_p_kernel(tc, x_words, x_scales, mem, w1, w2, offs, slo
         words = keep.tile([P, T], U32, name="words", align_bytes=64)
         scales = keep.tile([P, T], U8, name="scales", align_bytes=64)
         memory = keep.tile([P, U], F32, name="memory", align_bytes=64)
-        w2_raw = keep.tile([P, PACK, N], F32, name="w2_raw", tag="late2", align_bytes=64)
-        w1_raw = keep.tile([P, PACK, N], F32, name="w1_raw", tag="late1", align_bytes=64)
+        w2_raw = keep.tile([P, PACK, N], F32, name="w2_raw")
+        w1_raw = keep.tile([P, PACK, N], F32, name="w1_raw", tag="late", align_bytes=64)
         stacked = [keep.tile([P, n], U8, name="stacked%d" % h, align_bytes=64) for h, n in enumerate((EARLY, S - EARLY))]
         planes = [keep.tile([P, n], U8, name="plane%d" % h, align_bytes=64) for h, n in enumerate((EARLY, S - EARLY))]
 
@@ -48,7 +48,7 @@ def tile_picked_gmem_relu_p_kernel(tc, x_words, x_scales, mem, w1, w2, offs, slo
         for plane in planes:
             nc.vector.memset(plane[:].bitcast(I32), 0)
 
-        nc.sync.dma_start(scales[STACK:, :].bitcast(I32), x_scales[0].bitcast(I32))
+        nc.scalar.dma_start(scales[STACK:, :].bitcast(I32), x_scales[0].bitcast(I32))
         nc.sync.dma_start(offs_sb[:], offs)
         nc.sync.dma_start(words[:].bitcast(I32), x_words[0].rearrange("p n t -> p (n t)").bitcast(I32))
         nc.sync.dma_start(slot_sb[:], slot)
@@ -59,17 +59,17 @@ def tile_picked_gmem_relu_p_kernel(tc, x_words, x_scales, mem, w1, w2, offs, slo
         warm = keep.tile([P, 1], F32, name="warm")
         nc.scalar.activation(warm[:], w2_raw[:, 0, 0:1], ACT.Sigmoid)
 
-        def pick_scales(part, first, last):
+        def pick_scales(part, first, last, queues):
             nc.vector.tensor_copy(stacked[part][:], scales[:].indirect(offs_sb[:, entries(first, last)]))
-            for q in (0, 2, 1, 3):
-                nc.sync.dma_start(
+            for q, queue in zip((0, 2, 1, 3), queues):
+                queue.dma_start(
                     planes[part][32 * q : 32 * q + 4, :].bitcast(I32),
                     stacked[part][STACK + 4 * q : STACK + 4 * q + 4, :].bitcast(I32),
                 )
 
-        pick_scales(0, 0, EARLY)
+        pick_scales(0, 0, EARLY, (nc.sync,) * 4)
         nc.sync.dma_start(memory[:, MEM_FIRST:], mem[:, MEM_FIRST:])
-        pick_scales(1, EARLY, S)
+        pick_scales(1, EARLY, S, (nc.gpsimd, nc.sync, nc.sync, nc.sync))
 
         def quantise(grouped, name):
             codes = keep.tile([P, N], U32, name=name + "_codes", align_bytes=64)
@@ -78,13 +78,12 @@ def tile_picked_gmem_relu_p_kernel(tc, x_words, x_scales, mem, w1, w2, offs, slo
             return codes, plane
 
         def product(bank, base, weight, first, last):
-            tile, start = [(t, a) for t, a in picked if a <= first][-1]
             part, origin = (0, 0) if first < EARLY else (1, EARLY)
             nc.tensor.matmul_mx(
                 out=bank[:, first - base : last - base],
                 lhsT=weight[0][:].bitcast(FP8X4),
                 lhsT_scale=weight[1][:],
-                rhs=tile[:, first - start : last - start].bitcast(FP8X4),
+                rhs=picked[part][:, first - origin : last - origin].bitcast(FP8X4),
                 rhs_scale=planes[part][:, first - origin : last - origin],
                 start=True,
                 stop=True,
@@ -95,37 +94,37 @@ def tile_picked_gmem_relu_p_kernel(tc, x_words, x_scales, mem, w1, w2, offs, slo
         for grouped, raw in ((w2_grouped, w2_raw), (w1_grouped, w1_raw)):
             nc.scalar.copy(grouped[:].rearrange("p (c i) j -> p c j i", i=4), raw[:].rearrange("p j (c i) -> p c j i", i=4))
 
-        picked01 = keep.tile([P, HALF], U32, name="picked01", align_bytes=64)
-        nc.vector.tensor_copy(picked01[:], words[:].indirect(offs_sb[:, entries(0, HALF)]))
+        picked_early = keep.tile([P, EARLY], U32, name="picked_early", align_bytes=64)
+        nc.vector.tensor_copy(picked_early[:], words[:].indirect(offs_sb[:, entries(0, EARLY)]))
         w2_mx = quantise(w2_grouped, "w2")
-        picked2 = keep.tile([P, CHUNK], U32, name="picked2", tag="late2", align_bytes=64)
-        nc.vector.tensor_copy(picked2[:], words[:].indirect(offs_sb[:, entries(2 * CHUNK, 3 * CHUNK)]))
         w1_mx = quantise(w1_grouped, "w1")
-        picked3 = keep.tile([P, CHUNK], U32, name="picked3", tag="late1", align_bytes=64)
-        nc.vector.tensor_copy(picked3[:], words[:].indirect(offs_sb[:, entries(3 * CHUNK, S)]))
-        picked = [(picked01, 0), (picked2, 2 * CHUNK), (picked3, 3 * CHUNK)]
+        picked_late = keep.tile([P, S - EARLY], U32, name="picked_late", tag="late", align_bytes=64)
+        nc.vector.tensor_copy(picked_late[:], words[:].indirect(offs_sb[:, entries(EARLY, S)]))
+        picked = [picked_early, picked_late]
 
-        gate_parts = [(0, CHUNK), (CHUNK, EARLY), (EARLY, S)]
+        gate_parts = [(0, CHUNK), (CHUNK, EARLY), (EARLY, 3 * CHUNK), (3 * CHUNK, S)]
         cand_parts = [(0, CHUNK), (CHUNK, HALF), (HALF, S)]
         u2 = [psum.tile([P, b - a], F32, name="u2_%d" % a) for a, b in gate_parts]
         u1 = [psum.tile([P, b - a], F32, name="u1_%d" % a) for a, b in cand_parts]
         product(u2[0], 0, w2_mx, 0, CHUNK)
+        product(u1[0], 0, w1_mx, 0, CHUNK)
         product(u2[1], CHUNK, w2_mx, CHUNK, HALF)
         product(u2[1], CHUNK, w2_mx, HALF, EARLY)
-        product(u1[0], 0, w1_mx, 0, CHUNK)
         product(u1[1], CHUNK, w1_mx, CHUNK, HALF)
         product(u1[2], HALF, w1_mx, HALF, EARLY)
-        for bank, base, weight in ((u2[2], EARLY, w2_mx), (u1[2], HALF, w1_mx)):
-            product(bank, base, weight, EARLY, 3 * CHUNK)
-            product(bank, base, weight, 3 * CHUNK, S)
+        product(u2[2], EARLY, w2_mx, EARLY, 3 * CHUNK)
+        product(u2[3], 3 * CHUNK, w2_mx, 3 * CHUNK, S)
+        product(u1[2], HALF, w1_mx, EARLY, 3 * CHUNK)
+        product(u1[2], HALF, w1_mx, 3 * CHUNK, S)
 
         gate = keep.tile([P, S], F32, name="gate")
         cand = keep.tile([P, CHUNK], F32, name="cand")
         kept = keep.tile([P, S], F32, name="kept")
         taken = keep.tile([P, S], F32, name="taken")
         rest_first = keep.tile([P, CHUNK], F32, name="rest_first")
-        rest_last = keep.tile([P, S - EARLY], F32, name="rest_last")
-        rest = [rest_first[:], taken[:, CHUNK:EARLY], rest_last[:]]
+        rest_second = keep.tile([P, EARLY - CHUNK], F32, name="rest_second")
+        rest_last = keep.tile([P, CHUNK], F32, name="rest_last")
+        rest = [rest_first[:], rest_second[:], taken[:, HALF - 64 : HALF + 64], rest_last[:]]
 
         def factor(dst, part, sign):
             nc.scalar.activation(dst, u2[part][:], ACT.Sigmoid, scale=sign)
@@ -134,9 +133,11 @@ def tile_picked_gmem_relu_p_kernel(tc, x_words, x_scales, mem, w1, w2, offs, slo
         factor(rest[0], 0, -1.0)
         factor(rest[1], 1, -1.0)
         factor(gate[:, CHUNK:EARLY], 1, 1.0)
-        factor(rest[2], 2, -1.0)
         nc.scalar.activation(cand[:], u1[1][:], ACT.Relu)
-        factor(gate[:, EARLY:], 2, 1.0)
+        factor(rest[2], 2, -1.0)
+        factor(rest[3], 3, -1.0)
+        factor(gate[:, EARLY : 3 * CHUNK], 2, 1.0)
+        factor(gate[:, 3 * CHUNK :], 3, 1.0)
 
         nc.vector.scalar_tensor_tensor(taken[:, :CHUNK], u1[0][:], 0.0, gate[:, :CHUNK], ALU.max, ALU.mult)
         for part, (first, last) in enumerate(gate_parts):

@@ -22,7 +22,7 @@ STACK = P - ROWS
 CHUNK = 256
 EARLY = 640
 HALF = 512
-MEM_FIRST = 736
+MEM_FIRST = 640
 
 
 def tile_picked_gmem_relu_p_kernel(tc, x_words, x_scales, mem, w1, w2, offs, slot, out):
@@ -36,7 +36,7 @@ def tile_picked_gmem_relu_p_kernel(tc, x_words, x_scales, mem, w1, w2, offs, slo
         words = keep.tile([P, T], U32, name="words", align_bytes=64)
         scales = keep.tile([P, T], U8, name="scales", align_bytes=64)
         memory = keep.tile([P, U], F32, name="memory", align_bytes=64)
-        w2_raw = keep.tile([P, PACK, N], F32, name="w2_raw")
+        w2_raw = keep.tile([P, PACK, N], F32, name="w2_raw", tag="middle", align_bytes=64)
         w1_raw = keep.tile([P, PACK, N], F32, name="w1_raw", tag="late", align_bytes=64)
         stacked = [keep.tile([P, n], U8, name="stacked%d" % h, align_bytes=64) for h, n in enumerate((EARLY, S - EARLY))]
         planes = [keep.tile([P, n], U8, name="plane%d" % h, align_bytes=64) for h, n in enumerate((EARLY, S - EARLY))]
@@ -51,13 +51,14 @@ def tile_picked_gmem_relu_p_kernel(tc, x_words, x_scales, mem, w1, w2, offs, slo
         nc.scalar.dma_start(scales[STACK:, :].bitcast(I32), x_scales[0].bitcast(I32))
         nc.sync.dma_start(offs_sb[:], offs)
         nc.sync.dma_start(words[:].bitcast(I32), x_words[0].rearrange("p n t -> p (n t)").bitcast(I32))
-        nc.sync.dma_start(slot_sb[:], slot)
         nc.sync.dma_start(w2_raw[:], w2.rearrange("(p j) n -> p j n", j=PACK))
         nc.sync.dma_start(w1_raw[:], w1.rearrange("(p j) n -> p j n", j=PACK))
         nc.sync.dma_start(memory[:, :MEM_FIRST], mem[:, :MEM_FIRST])
 
         warm = keep.tile([P, 1], F32, name="warm")
-        nc.scalar.activation(warm[:], w2_raw[:, 0, 0:1], ACT.Sigmoid)
+        zero = keep.tile([P, 1], F32, name="zero")
+        nc.gpsimd.memset(zero[:], 0.0)
+        nc.scalar.activation(warm[:], zero[:], ACT.Sigmoid)
 
         def pick_scales(part, first, last, queues):
             nc.vector.tensor_copy(stacked[part][:], scales[:].indirect(offs_sb[:, entries(first, last)]))
@@ -67,8 +68,9 @@ def tile_picked_gmem_relu_p_kernel(tc, x_words, x_scales, mem, w1, w2, offs, slo
                     stacked[part][STACK + 4 * q : STACK + 4 * q + 4, :].bitcast(I32),
                 )
 
-        pick_scales(0, 0, EARLY, (nc.sync,) * 4)
+        pick_scales(0, 0, EARLY, (nc.sync, nc.scalar, nc.sync, nc.scalar))
         nc.sync.dma_start(memory[:, MEM_FIRST:], mem[:, MEM_FIRST:])
+        nc.sync.dma_start(slot_sb[:], slot)
         pick_scales(1, EARLY, S, (nc.gpsimd, nc.sync, nc.sync, nc.sync))
 
         def quantise(grouped, name):
@@ -78,12 +80,13 @@ def tile_picked_gmem_relu_p_kernel(tc, x_words, x_scales, mem, w1, w2, offs, slo
             return codes, plane
 
         def product(bank, base, weight, first, last):
+            tile, start = [(t, a) for t, a in picked if a <= first][-1]
             part, origin = (0, 0) if first < EARLY else (1, EARLY)
             nc.tensor.matmul_mx(
                 out=bank[:, first - base : last - base],
                 lhsT=weight[0][:].bitcast(FP8X4),
                 lhsT_scale=weight[1][:],
-                rhs=picked[part][:, first - origin : last - origin].bitcast(FP8X4),
+                rhs=tile[:, first - start : last - start].bitcast(FP8X4),
                 rhs_scale=planes[part][:, first - origin : last - origin],
                 start=True,
                 stop=True,
@@ -94,13 +97,18 @@ def tile_picked_gmem_relu_p_kernel(tc, x_words, x_scales, mem, w1, w2, offs, slo
         for grouped, raw in ((w2_grouped, w2_raw), (w1_grouped, w1_raw)):
             nc.scalar.copy(grouped[:].rearrange("p (c i) j -> p c j i", i=4), raw[:].rearrange("p j (c i) -> p c j i", i=4))
 
-        picked_early = keep.tile([P, EARLY], U32, name="picked_early", align_bytes=64)
-        nc.vector.tensor_copy(picked_early[:], words[:].indirect(offs_sb[:, entries(0, EARLY)]))
+        picked = []
+
+        def pick_words(first, last, **place):
+            tile = keep.tile([P, last - first], U32, name="picked%d" % first, align_bytes=64, **place)
+            nc.vector.tensor_copy(tile[:], words[:].indirect(offs_sb[:, entries(first, last)]))
+            picked.append((tile, first))
+
+        pick_words(0, EARLY - CHUNK)
         w2_mx = quantise(w2_grouped, "w2")
+        pick_words(EARLY - CHUNK, EARLY, tag="middle")
         w1_mx = quantise(w1_grouped, "w1")
-        picked_late = keep.tile([P, S - EARLY], U32, name="picked_late", tag="late", align_bytes=64)
-        nc.vector.tensor_copy(picked_late[:], words[:].indirect(offs_sb[:, entries(EARLY, S)]))
-        picked = [picked_early, picked_late]
+        pick_words(EARLY, S, tag="late")
 
         gate_parts = [(0, CHUNK), (CHUNK, EARLY), (EARLY, 3 * CHUNK), (3 * CHUNK, S)]
         cand_parts = [(0, CHUNK), (CHUNK, HALF), (HALF, S)]
@@ -108,9 +116,10 @@ def tile_picked_gmem_relu_p_kernel(tc, x_words, x_scales, mem, w1, w2, offs, slo
         u1 = [psum.tile([P, b - a], F32, name="u1_%d" % a) for a, b in cand_parts]
         product(u2[0], 0, w2_mx, 0, CHUNK)
         product(u1[0], 0, w1_mx, 0, CHUNK)
-        product(u2[1], CHUNK, w2_mx, CHUNK, HALF)
-        product(u2[1], CHUNK, w2_mx, HALF, EARLY)
-        product(u1[1], CHUNK, w1_mx, CHUNK, HALF)
+        product(u2[1], CHUNK, w2_mx, CHUNK, EARLY - CHUNK)
+        product(u2[1], CHUNK, w2_mx, EARLY - CHUNK, EARLY)
+        product(u1[1], CHUNK, w1_mx, CHUNK, EARLY - CHUNK)
+        product(u1[1], CHUNK, w1_mx, EARLY - CHUNK, HALF)
         product(u1[2], HALF, w1_mx, HALF, EARLY)
         product(u2[2], EARLY, w2_mx, EARLY, 3 * CHUNK)
         product(u2[3], 3 * CHUNK, w2_mx, 3 * CHUNK, S)

@@ -22,7 +22,7 @@ STACK = P - ROWS
 CHUNK = 256
 EARLY = 640
 HALF = 512
-MEM_FIRST = 640
+MEM_FIRST = 704
 
 
 def tile_picked_gmem_relu_p_kernel(tc, x_words, x_scales, mem, w1, w2, offs, slot, out):
@@ -36,7 +36,7 @@ def tile_picked_gmem_relu_p_kernel(tc, x_words, x_scales, mem, w1, w2, offs, slo
         words = keep.tile([P, T], U32, name="words", align_bytes=64)
         scales = keep.tile([P, T], U8, name="scales", align_bytes=64)
         memory = keep.tile([P, U], F32, name="memory", align_bytes=64)
-        w2_raw = keep.tile([P, PACK, N], F32, name="w2_raw", tag="middle", align_bytes=64)
+        w2_raw = keep.tile([P, PACK, N], F32, name="w2_raw")
         w1_raw = keep.tile([P, PACK, N], F32, name="w1_raw", tag="late", align_bytes=64)
         stacked = [keep.tile([P, n], U8, name="stacked%d" % h, align_bytes=64) for h, n in enumerate((EARLY, S - EARLY))]
         planes = [keep.tile([P, n], U8, name="plane%d" % h, align_bytes=64) for h, n in enumerate((EARLY, S - EARLY))]
@@ -57,7 +57,7 @@ def tile_picked_gmem_relu_p_kernel(tc, x_words, x_scales, mem, w1, w2, offs, slo
 
         warm = keep.tile([P, 1], F32, name="warm")
         zero = keep.tile([P, 1], F32, name="zero")
-        nc.gpsimd.memset(zero[:], 0.0)
+        nc.vector.memset(zero[:], 0.0)
         nc.scalar.activation(warm[:], zero[:], ACT.Sigmoid)
 
         def pick_scales(part, first, last, queues):
@@ -104,9 +104,8 @@ def tile_picked_gmem_relu_p_kernel(tc, x_words, x_scales, mem, w1, w2, offs, slo
             nc.vector.tensor_copy(tile[:], words[:].indirect(offs_sb[:, entries(first, last)]))
             picked.append((tile, first))
 
-        pick_words(0, EARLY - CHUNK)
+        pick_words(0, EARLY)
         w2_mx = quantise(w2_grouped, "w2")
-        pick_words(EARLY - CHUNK, EARLY, tag="middle")
         w1_mx = quantise(w1_grouped, "w1")
         pick_words(EARLY, S, tag="late")
 
@@ -116,10 +115,9 @@ def tile_picked_gmem_relu_p_kernel(tc, x_words, x_scales, mem, w1, w2, offs, slo
         u1 = [psum.tile([P, b - a], F32, name="u1_%d" % a) for a, b in cand_parts]
         product(u2[0], 0, w2_mx, 0, CHUNK)
         product(u1[0], 0, w1_mx, 0, CHUNK)
-        product(u2[1], CHUNK, w2_mx, CHUNK, EARLY - CHUNK)
-        product(u2[1], CHUNK, w2_mx, EARLY - CHUNK, EARLY)
-        product(u1[1], CHUNK, w1_mx, CHUNK, EARLY - CHUNK)
-        product(u1[1], CHUNK, w1_mx, EARLY - CHUNK, HALF)
+        product(u2[1], CHUNK, w2_mx, CHUNK, HALF)
+        product(u2[1], CHUNK, w2_mx, HALF, EARLY)
+        product(u1[1], CHUNK, w1_mx, CHUNK, HALF)
         product(u1[2], HALF, w1_mx, HALF, EARLY)
         product(u2[2], EARLY, w2_mx, EARLY, 3 * CHUNK)
         product(u2[3], 3 * CHUNK, w2_mx, 3 * CHUNK, S)

@@ -22,7 +22,8 @@ STACK = P - ROWS
 CHUNK = 256
 EARLY = 640
 HALF = 512
-MEM_FIRST = 704
+SPLIT = 448
+MEM_FIRST = 512
 
 
 def tile_picked_gmem_relu_p_kernel(tc, x_words, x_scales, mem, w1, w2, offs, slot, out):
@@ -60,18 +61,23 @@ def tile_picked_gmem_relu_p_kernel(tc, x_words, x_scales, mem, w1, w2, offs, slo
         nc.vector.memset(zero[:], 0.0)
         nc.scalar.activation(warm[:], zero[:], ACT.Sigmoid)
 
-        def pick_scales(part, first, last, queues):
+        def pick_scales(part, first, last):
             nc.vector.tensor_copy(stacked[part][:], scales[:].indirect(offs_sb[:, entries(first, last)]))
-            for q, queue in zip((0, 2, 1, 3), queues):
+
+        def move_scales(part, quadrants, queues):
+            for q, queue in zip(quadrants, queues):
                 queue.dma_start(
                     planes[part][32 * q : 32 * q + 4, :].bitcast(I32),
                     stacked[part][STACK + 4 * q : STACK + 4 * q + 4, :].bitcast(I32),
                 )
 
-        pick_scales(0, 0, EARLY, (nc.sync, nc.scalar, nc.sync, nc.scalar))
+        pick_scales(0, 0, EARLY)
+        move_scales(0, (0, 2, 1, 3), (nc.sync, nc.scalar, nc.sync, nc.scalar))
         nc.sync.dma_start(memory[:, MEM_FIRST:], mem[:, MEM_FIRST:])
+        pick_scales(1, EARLY, S)
+        move_scales(1, (0, 2, 1), (nc.gpsimd, nc.sync, nc.sync))
         nc.sync.dma_start(slot_sb[:], slot)
-        pick_scales(1, EARLY, S, (nc.gpsimd, nc.sync, nc.sync, nc.sync))
+        move_scales(1, (3,), (nc.sync,))
 
         def quantise(grouped, name):
             codes = keep.tile([P, N], U32, name=name + "_codes", align_bytes=64)
@@ -109,49 +115,49 @@ def tile_picked_gmem_relu_p_kernel(tc, x_words, x_scales, mem, w1, w2, offs, slo
         w1_mx = quantise(w1_grouped, "w1")
         pick_words(EARLY, S, tag="late")
 
-        gate_parts = [(0, CHUNK), (CHUNK, EARLY), (EARLY, 3 * CHUNK), (3 * CHUNK, S)]
-        cand_parts = [(0, CHUNK), (CHUNK, HALF), (HALF, S)]
+        gate_parts = [(0, CHUNK), (CHUNK, EARLY), (EARLY, S)]
         u2 = [psum.tile([P, b - a], F32, name="u2_%d" % a) for a, b in gate_parts]
-        u1 = [psum.tile([P, b - a], F32, name="u1_%d" % a) for a, b in cand_parts]
+        u1 = [psum.tile([P, b - a], F32, name="u1_%d" % a) for a, b in gate_parts]
         product(u2[0], 0, w2_mx, 0, CHUNK)
-        product(u1[0], 0, w1_mx, 0, CHUNK)
         product(u2[1], CHUNK, w2_mx, CHUNK, HALF)
         product(u2[1], CHUNK, w2_mx, HALF, EARLY)
-        product(u1[1], CHUNK, w1_mx, CHUNK, HALF)
-        product(u1[2], HALF, w1_mx, HALF, EARLY)
+        product(u1[0], 0, w1_mx, 0, CHUNK)
         product(u2[2], EARLY, w2_mx, EARLY, 3 * CHUNK)
-        product(u2[3], 3 * CHUNK, w2_mx, 3 * CHUNK, S)
-        product(u1[2], HALF, w1_mx, EARLY, 3 * CHUNK)
-        product(u1[2], HALF, w1_mx, 3 * CHUNK, S)
+        product(u2[2], EARLY, w2_mx, 3 * CHUNK, S)
+        product(u1[1], CHUNK, w1_mx, CHUNK, HALF)
+        product(u1[1], CHUNK, w1_mx, HALF, EARLY)
+        product(u1[2], EARLY, w1_mx, EARLY, 3 * CHUNK)
+        product(u1[2], EARLY, w1_mx, 3 * CHUNK, S)
+
+        def looked_up(first, last):
+            return memory[:].indirect(slot_sb[:, entries(first, last)])
 
         gate = keep.tile([P, S], F32, name="gate")
-        cand = keep.tile([P, CHUNK], F32, name="cand")
-        kept = keep.tile([P, S], F32, name="kept")
-        taken = keep.tile([P, S], F32, name="taken")
-        rest_first = keep.tile([P, CHUNK], F32, name="rest_first")
-        rest_second = keep.tile([P, EARLY - CHUNK], F32, name="rest_second")
-        rest_last = keep.tile([P, CHUNK], F32, name="rest_last")
-        rest = [rest_first[:], rest_second[:], taken[:, HALF - 64 : HALF + 64], rest_last[:]]
+        rest = keep.tile([P, CHUNK], F32, name="rest")
+        nc.scalar.activation(rest[:], u2[0][:], ACT.Sigmoid, scale=-1.0)
+        nc.scalar.activation(gate[:, :CHUNK], u2[0][:], ACT.Sigmoid)
+        nc.scalar.activation(gate[:, CHUNK:EARLY], u2[1][:], ACT.Sigmoid)
 
-        def factor(dst, part, sign):
-            nc.scalar.activation(dst, u2[part][:], ACT.Sigmoid, scale=sign)
+        taken = keep.tile([P, CHUNK], F32, name="taken")
+        kept = keep.tile([P, CHUNK], F32, name="kept")
+        new = keep.tile([P, CHUNK], F32, name="new")
+        old = keep.tile([P, S - CHUNK], F32, name="old")
+        nc.vector.scalar_tensor_tensor(taken[:], u1[0][:], 0.0, gate[:, :CHUNK], ALU.max, ALU.mult)
+        nc.vector.tensor_tensor(kept[:], looked_up(0, CHUNK), rest[:], ALU.mult)
+        nc.vector.tensor_copy(old[:, : SPLIT - CHUNK], looked_up(CHUNK, SPLIT))
+        nc.scalar.activation(old[:, SPLIT - CHUNK :], looked_up(SPLIT, S), ACT.Copy)
+        nc.scalar.activation(gate[:, EARLY:], u2[2][:], ACT.Sigmoid)
+        nc.vector.tensor_tensor(new[:], taken[:], kept[:], ALU.add)
+        nc.scalar.activation(looked_up(0, CHUNK), new[:], ACT.Copy)
 
-        factor(gate[:, :CHUNK], 0, 1.0)
-        factor(rest[0], 0, -1.0)
-        factor(rest[1], 1, -1.0)
-        factor(gate[:, CHUNK:EARLY], 1, 1.0)
-        nc.scalar.activation(cand[:], u1[1][:], ACT.Relu)
-        factor(rest[2], 2, -1.0)
-        factor(rest[3], 3, -1.0)
-        factor(gate[:, EARLY : 3 * CHUNK], 2, 1.0)
-        factor(gate[:, 3 * CHUNK :], 3, 1.0)
-
-        nc.vector.scalar_tensor_tensor(taken[:, :CHUNK], u1[0][:], 0.0, gate[:, :CHUNK], ALU.max, ALU.mult)
-        for part, (first, last) in enumerate(gate_parts):
-            nc.vector.tensor_tensor(kept[:, first:last], memory[:].indirect(slot_sb[:, entries(first, last)]), rest[part], ALU.mult)
-
-        nc.gpsimd.tensor_tensor(taken[:, CHUNK:HALF], cand[:], gate[:, CHUNK:HALF], ALU.mult)
-        nc.vector.scalar_tensor_tensor(taken[:, HALF:], u1[2][:], 0.0, gate[:, HALF:], ALU.max, ALU.mult)
-        nc.vector.tensor_tensor(memory[:].indirect(slot_sb[:]), taken[:], kept[:], ALU.add)
+        away = keep.tile([P, S - CHUNK], F32, name="away")
+        step = keep.tile([P, S - CHUNK], F32, name="step")
+        for bank, (first, last) in zip(u1[1:], gate_parts[1:]):
+            part = slice(first - CHUNK, last - CHUNK)
+            nc.vector.scalar_tensor_tensor(away[:, part], bank[:], 0.0, old[:, part], ALU.max, ALU.subtract)
+        for first, last in gate_parts[1:]:
+            part = slice(first - CHUNK, last - CHUNK)
+            nc.vector.tensor_tensor(step[:, part], away[:, part], gate[:, first:last], ALU.mult)
+        nc.vector.tensor_tensor(looked_up(CHUNK, S), step[:], old[:], ALU.add)
 
         nc.sync.dma_start(out, memory[:])

@@ -19,17 +19,18 @@ P = 128
 PACK = 4
 ROWS = 16
 STACK = P - ROWS
-CHUNK = 256
 EARLY = 640
-HALF = 512
-SPLIT = 448
 MEM_FIRST = 512
+FIRST = 256
+SPLIT = 480
+HALF = 512
 
 
 def tile_picked_gmem_relu_p_kernel(tc, x_words, x_scales, mem, w1, w2, offs, slot, out):
     nc = tc.nc
     with ExitStack() as ctx:
         keep = ctx.enter_context(tc.tile_pool(name="keep", bufs=1))
+        reuse = ctx.enter_context(tc.tile_pool(name="reuse", bufs=1))
         psum = ctx.enter_context(tc.psum_pool(name="psum", bufs=1))
 
         offs_sb = keep.tile([P, S // 16], U16, name="offs_sb")
@@ -37,9 +38,12 @@ def tile_picked_gmem_relu_p_kernel(tc, x_words, x_scales, mem, w1, w2, offs, slo
         words = keep.tile([P, T], U32, name="words", align_bytes=64)
         scales = keep.tile([P, T], U8, name="scales", align_bytes=64)
         memory = keep.tile([P, U], F32, name="memory", align_bytes=64)
-        w2_raw = keep.tile([P, PACK, N], F32, name="w2_raw")
-        w1_raw = keep.tile([P, PACK, N], F32, name="w1_raw", tag="late", align_bytes=64)
-        stacked = [keep.tile([P, n], U8, name="stacked%d" % h, align_bytes=64) for h, n in enumerate((EARLY, S - EARLY))]
+        w2_raw = keep.tile([P, PACK, N], F32, name="w2_raw", tag="after_w2", align_bytes=64)
+        w1_raw = keep.tile([P, PACK, N], F32, name="w1_raw", tag="after_w1", align_bytes=64)
+        stacked = [
+            keep.tile([P, EARLY], U8, name="stacked_early", align_bytes=64),
+            reuse.tile([P, S - EARLY], U8, name="stacked_late", offset=4 * FIRST - 128, align_bytes=64),
+        ]
         planes = [keep.tile([P, n], U8, name="plane%d" % h, align_bytes=64) for h, n in enumerate((EARLY, S - EARLY))]
 
         def entries(first, last):
@@ -74,16 +78,30 @@ def tile_picked_gmem_relu_p_kernel(tc, x_words, x_scales, mem, w1, w2, offs, slo
         pick_scales(0, 0, EARLY)
         move_scales(0, (0, 2, 1, 3), (nc.sync, nc.scalar, nc.sync, nc.scalar))
         nc.sync.dma_start(memory[:, MEM_FIRST:], mem[:, MEM_FIRST:])
-        pick_scales(1, EARLY, S)
-        move_scales(1, (0, 2, 1), (nc.gpsimd, nc.sync, nc.sync))
         nc.sync.dma_start(slot_sb[:], slot)
-        move_scales(1, (3,), (nc.sync,))
+        pick_scales(1, EARLY, S)
+        move_scales(1, (0, 2, 1, 3), (nc.gpsimd, nc.sync, nc.sync, nc.sync))
 
-        def quantise(grouped, name):
+        def quantise(raw, name):
+            grouped = keep.tile([P, N, PACK], BF16, name=name + "_grouped", align_bytes=64)
+            nc.scalar.copy(grouped[:].rearrange("p (c i) j -> p c j i", i=4), raw[:].rearrange("p j (c i) -> p c j i", i=4))
             codes = keep.tile([P, N], U32, name=name + "_codes", align_bytes=64)
-            plane = keep.tile([P, N], U8, name=name + "_scales", align_bytes=64)
-            nc.vector.quantize_mx(out=codes[:].bitcast(FP8X4), scales=plane[:], in_=grouped[:].rearrange("p n j -> p (n j)"))
-            return codes, plane
+            bytes_ = keep.tile([P, N], U8, name=name + "_scales", align_bytes=64)
+            nc.vector.quantize_mx(out=codes[:].bitcast(FP8X4), scales=bytes_[:], in_=grouped[:].rearrange("p n j -> p (n j)"))
+            return codes, bytes_
+
+        picked = []
+
+        def pick_words(first, last, **place):
+            tile = keep.tile([P, last - first], U32, name="picked%d" % first, align_bytes=64, **place)
+            nc.vector.tensor_copy(tile[:], words[:].indirect(offs_sb[:, entries(first, last)]))
+            picked.append((tile, first))
+
+        pick_words(0, HALF)
+        w2_mx = quantise(w2_raw, "w2")
+        pick_words(HALF, 768, tag="after_w2")
+        w1_mx = quantise(w1_raw, "w1")
+        pick_words(768, S, tag="after_w1")
 
         def product(bank, base, weight, first, last):
             tile, start = [(t, a) for t, a in picked if a <= first][-1]
@@ -98,66 +116,56 @@ def tile_picked_gmem_relu_p_kernel(tc, x_words, x_scales, mem, w1, w2, offs, slo
                 stop=True,
             )
 
-        w2_grouped = keep.tile([P, N, PACK], BF16, name="w2_grouped", align_bytes=64)
-        w1_grouped = keep.tile([P, N, PACK], BF16, name="w1_grouped", align_bytes=64)
-        for grouped, raw in ((w2_grouped, w2_raw), (w1_grouped, w1_raw)):
-            nc.scalar.copy(grouped[:].rearrange("p (c i) j -> p c j i", i=4), raw[:].rearrange("p j (c i) -> p c j i", i=4))
-
-        picked = []
-
-        def pick_words(first, last, **place):
-            tile = keep.tile([P, last - first], U32, name="picked%d" % first, align_bytes=64, **place)
-            nc.vector.tensor_copy(tile[:], words[:].indirect(offs_sb[:, entries(first, last)]))
-            picked.append((tile, first))
-
-        pick_words(0, EARLY)
-        w2_mx = quantise(w2_grouped, "w2")
-        w1_mx = quantise(w1_grouped, "w1")
-        pick_words(EARLY, S, tag="late")
-
-        gate_parts = [(0, CHUNK), (CHUNK, EARLY), (EARLY, S)]
+        gate_parts = [(0, FIRST), (FIRST, EARLY), (EARLY, 768), (768, S)]
+        cand_parts = [(0, FIRST), (FIRST, EARLY), (EARLY, S)]
         u2 = [psum.tile([P, b - a], F32, name="u2_%d" % a) for a, b in gate_parts]
-        u1 = [psum.tile([P, b - a], F32, name="u1_%d" % a) for a, b in gate_parts]
-        product(u2[0], 0, w2_mx, 0, CHUNK)
-        product(u2[1], CHUNK, w2_mx, CHUNK, HALF)
-        product(u2[1], CHUNK, w2_mx, HALF, EARLY)
-        product(u1[0], 0, w1_mx, 0, CHUNK)
-        product(u2[2], EARLY, w2_mx, EARLY, 3 * CHUNK)
-        product(u2[2], EARLY, w2_mx, 3 * CHUNK, S)
-        product(u1[1], CHUNK, w1_mx, CHUNK, HALF)
-        product(u1[1], CHUNK, w1_mx, HALF, EARLY)
-        product(u1[2], EARLY, w1_mx, EARLY, 3 * CHUNK)
-        product(u1[2], EARLY, w1_mx, 3 * CHUNK, S)
+        u1 = [psum.tile([P, b - a], F32, name="u1_%d" % a) for a, b in cand_parts]
+        product(u2[0], 0, w2_mx, 0, FIRST)
+        product(u2[1], FIRST, w2_mx, FIRST, HALF)
+        product(u2[1], FIRST, w2_mx, HALF, EARLY)
+        product(u1[0], 0, w1_mx, 0, FIRST)
+        product(u1[1], FIRST, w1_mx, FIRST, HALF)
+        product(u1[1], FIRST, w1_mx, HALF, EARLY)
+        for bank, (first, last) in zip(u2[2:], gate_parts[2:]):
+            product(bank, first, w2_mx, first, last)
+        product(u1[2], EARLY, w1_mx, EARLY, 768)
+        product(u1[2], EARLY, w1_mx, 768, S)
 
         def looked_up(first, last):
             return memory[:].indirect(slot_sb[:, entries(first, last)])
 
         gate = keep.tile([P, S], F32, name="gate")
-        rest = keep.tile([P, CHUNK], F32, name="rest")
+        rest = keep.tile([P, FIRST], F32, name="rest")
+
+        def make_gate(part):
+            first, last = gate_parts[part]
+            nc.scalar.activation(gate[:, first:last], u2[part][:], ACT.Sigmoid)
+
+        make_gate(0)
         nc.scalar.activation(rest[:], u2[0][:], ACT.Sigmoid, scale=-1.0)
-        nc.scalar.activation(gate[:, :CHUNK], u2[0][:], ACT.Sigmoid)
-        nc.scalar.activation(gate[:, CHUNK:EARLY], u2[1][:], ACT.Sigmoid)
+        make_gate(1)
 
-        taken = keep.tile([P, CHUNK], F32, name="taken")
-        kept = keep.tile([P, CHUNK], F32, name="kept")
-        new = keep.tile([P, CHUNK], F32, name="new")
-        old = keep.tile([P, S - CHUNK], F32, name="old")
-        nc.vector.scalar_tensor_tensor(taken[:], u1[0][:], 0.0, gate[:, :CHUNK], ALU.max, ALU.mult)
-        nc.vector.tensor_tensor(kept[:], looked_up(0, CHUNK), rest[:], ALU.mult)
-        nc.vector.tensor_copy(old[:, : SPLIT - CHUNK], looked_up(CHUNK, SPLIT))
-        nc.scalar.activation(old[:, SPLIT - CHUNK :], looked_up(SPLIT, S), ACT.Copy)
-        nc.scalar.activation(gate[:, EARLY:], u2[2][:], ACT.Sigmoid)
+        taken = keep.tile([P, FIRST], F32, name="taken")
+        kept = keep.tile([P, FIRST], F32, name="kept")
+        new = reuse.tile([P, FIRST], F32, name="new", offset=0)
+        old = keep.tile([P, S - FIRST], F32, name="old")
+        nc.vector.scalar_tensor_tensor(taken[:], u1[0][:], 0.0, gate[:, :FIRST], ALU.max, ALU.mult)
+        nc.vector.tensor_tensor(kept[:], looked_up(0, FIRST), rest[:], ALU.mult)
+        nc.vector.tensor_copy(old[:, : SPLIT - FIRST], looked_up(FIRST, SPLIT))
+        nc.scalar.activation(old[:, SPLIT - FIRST :], looked_up(SPLIT, S), ACT.Copy)
+        for part in range(2, len(gate_parts)):
+            make_gate(part)
         nc.vector.tensor_tensor(new[:], taken[:], kept[:], ALU.add)
-        nc.scalar.activation(looked_up(0, CHUNK), new[:], ACT.Copy)
+        nc.scalar.activation(looked_up(0, FIRST), new[:], ACT.Copy)
 
-        away = keep.tile([P, S - CHUNK], F32, name="away")
-        step = keep.tile([P, S - CHUNK], F32, name="step")
-        for bank, (first, last) in zip(u1[1:], gate_parts[1:]):
-            part = slice(first - CHUNK, last - CHUNK)
+        away = reuse.tile([P, S - FIRST], F32, name="away", offset=4 * FIRST)
+        step = keep.tile([P, S - FIRST], F32, name="step")
+        for bank, (first, last) in zip(u1[1:], cand_parts[1:]):
+            part = slice(first - FIRST, last - FIRST)
             nc.vector.scalar_tensor_tensor(away[:, part], bank[:], 0.0, old[:, part], ALU.max, ALU.subtract)
-        for first, last in gate_parts[1:]:
-            part = slice(first - CHUNK, last - CHUNK)
+        for first, last in cand_parts[1:]:
+            part = slice(first - FIRST, last - FIRST)
             nc.vector.tensor_tensor(step[:, part], away[:, part], gate[:, first:last], ALU.mult)
-        nc.vector.tensor_tensor(looked_up(CHUNK, S), step[:], old[:], ALU.add)
+        nc.vector.tensor_tensor(looked_up(FIRST, S), step[:], old[:], ALU.add)
 
         nc.sync.dma_start(out, memory[:])

@@ -17,13 +17,18 @@ ALU = mybir.AluOpType
 
 P = 128
 PACK = 4
-ROWS = 16
-STACK = P - ROWS
+LIST_ROWS = 16
+BLOCKS = 16
+STACK = P - BLOCKS
+QUADRANT = 32
+F32_BYTES = 4
+
 EARLY = 640
 MEM_FIRST = 512
 FIRST = 256
-SPLIT = 480
-HALF = 512
+SPLIT = 448
+WORDS_A, WORDS_B = 512, 768
+SHARED = 128
 
 
 def tile_picked_gmem_relu_p_kernel(tc, x_words, x_scales, mem, w1, w2, offs, slot, out):
@@ -33,8 +38,8 @@ def tile_picked_gmem_relu_p_kernel(tc, x_words, x_scales, mem, w1, w2, offs, slo
         reuse = ctx.enter_context(tc.tile_pool(name="reuse", bufs=1))
         psum = ctx.enter_context(tc.psum_pool(name="psum", bufs=1))
 
-        offs_sb = keep.tile([P, S // 16], U16, name="offs_sb")
-        slot_sb = keep.tile([P, S // 16], U16, name="slot_sb")
+        offs_sb = keep.tile([P, S // LIST_ROWS], U16, name="offs_sb")
+        slot_sb = keep.tile([P, S // LIST_ROWS], U16, name="slot_sb")
         words = keep.tile([P, T], U32, name="words", align_bytes=64)
         scales = keep.tile([P, T], U8, name="scales", align_bytes=64)
         memory = keep.tile([P, U], F32, name="memory", align_bytes=64)
@@ -42,12 +47,12 @@ def tile_picked_gmem_relu_p_kernel(tc, x_words, x_scales, mem, w1, w2, offs, slo
         w1_raw = keep.tile([P, PACK, N], F32, name="w1_raw", tag="after_w1", align_bytes=64)
         stacked = [
             keep.tile([P, EARLY], U8, name="stacked_early", align_bytes=64),
-            reuse.tile([P, S - EARLY], U8, name="stacked_late", offset=4 * FIRST - 128, align_bytes=64),
+            reuse.tile([P, S - EARLY], U8, name="stacked_late", offset=F32_BYTES * FIRST - SHARED, align_bytes=64),
         ]
         planes = [keep.tile([P, n], U8, name="plane%d" % h, align_bytes=64) for h, n in enumerate((EARLY, S - EARLY))]
 
         def entries(first, last):
-            return slice(first // 16, last // 16)
+            return slice(first // LIST_ROWS, last // LIST_ROWS)
 
         nc.vector.memset(scales[:STACK, :].bitcast(I32), 0)
         for plane in planes:
@@ -65,30 +70,26 @@ def tile_picked_gmem_relu_p_kernel(tc, x_words, x_scales, mem, w1, w2, offs, slo
         nc.vector.memset(zero[:], 0.0)
         nc.scalar.activation(warm[:], zero[:], ACT.Sigmoid)
 
-        def pick_scales(part, first, last):
+        def pick_scales(part, first, last, queues):
             nc.vector.tensor_copy(stacked[part][:], scales[:].indirect(offs_sb[:, entries(first, last)]))
-
-        def move_scales(part, quadrants, queues):
-            for q, queue in zip(quadrants, queues):
+            for q, queue in zip((0, 2, 1, 3), queues):
                 queue.dma_start(
-                    planes[part][32 * q : 32 * q + 4, :].bitcast(I32),
+                    planes[part][QUADRANT * q : QUADRANT * q + 4, :].bitcast(I32),
                     stacked[part][STACK + 4 * q : STACK + 4 * q + 4, :].bitcast(I32),
                 )
 
-        pick_scales(0, 0, EARLY)
-        move_scales(0, (0, 2, 1, 3), (nc.sync, nc.scalar, nc.sync, nc.scalar))
+        pick_scales(0, 0, EARLY, (nc.sync, nc.scalar, nc.sync, nc.scalar))
         nc.sync.dma_start(memory[:, MEM_FIRST:], mem[:, MEM_FIRST:])
         nc.sync.dma_start(slot_sb[:], slot)
-        pick_scales(1, EARLY, S)
-        move_scales(1, (0, 2, 1, 3), (nc.gpsimd, nc.sync, nc.sync, nc.sync))
+        pick_scales(1, EARLY, S, (nc.gpsimd, nc.sync, nc.sync, nc.sync))
 
         def quantise(raw, name):
             grouped = keep.tile([P, N, PACK], BF16, name=name + "_grouped", align_bytes=64)
             nc.scalar.copy(grouped[:].rearrange("p (c i) j -> p c j i", i=4), raw[:].rearrange("p j (c i) -> p c j i", i=4))
             codes = keep.tile([P, N], U32, name=name + "_codes", align_bytes=64)
-            bytes_ = keep.tile([P, N], U8, name=name + "_scales", align_bytes=64)
-            nc.vector.quantize_mx(out=codes[:].bitcast(FP8X4), scales=bytes_[:], in_=grouped[:].rearrange("p n j -> p (n j)"))
-            return codes, bytes_
+            plane = keep.tile([P, N], U8, name=name + "_scales", align_bytes=64)
+            nc.vector.quantize_mx(out=codes[:].bitcast(FP8X4), scales=plane[:], in_=grouped[:].rearrange("p n j -> p (n j)"))
+            return codes, plane
 
         picked = []
 
@@ -97,11 +98,11 @@ def tile_picked_gmem_relu_p_kernel(tc, x_words, x_scales, mem, w1, w2, offs, slo
             nc.vector.tensor_copy(tile[:], words[:].indirect(offs_sb[:, entries(first, last)]))
             picked.append((tile, first))
 
-        pick_words(0, HALF)
+        pick_words(0, WORDS_A)
         w2_mx = quantise(w2_raw, "w2")
-        pick_words(HALF, 768, tag="after_w2")
+        pick_words(WORDS_A, WORDS_B, tag="after_w2")
         w1_mx = quantise(w1_raw, "w1")
-        pick_words(768, S, tag="after_w1")
+        pick_words(WORDS_B, S, tag="after_w1")
 
         def product(bank, base, weight, first, last):
             tile, start = [(t, a) for t, a in picked if a <= first][-1]
@@ -116,22 +117,19 @@ def tile_picked_gmem_relu_p_kernel(tc, x_words, x_scales, mem, w1, w2, offs, slo
                 stop=True,
             )
 
-        gate_parts = [(0, FIRST), (FIRST, EARLY), (EARLY, 768), (768, S)]
+        gate_parts = [(0, FIRST), (FIRST, EARLY), (EARLY, S)]
         cand_parts = [(0, FIRST), (FIRST, EARLY), (EARLY, S)]
         u2 = [psum.tile([P, b - a], F32, name="u2_%d" % a) for a, b in gate_parts]
         u1 = [psum.tile([P, b - a], F32, name="u1_%d" % a) for a, b in cand_parts]
-        product(u2[0], 0, w2_mx, 0, FIRST)
-        product(u2[1], FIRST, w2_mx, FIRST, HALF)
-        product(u2[1], FIRST, w2_mx, HALF, EARLY)
-        product(u1[0], 0, w1_mx, 0, FIRST)
-        product(u1[1], FIRST, w1_mx, FIRST, HALF)
-        product(u1[1], FIRST, w1_mx, HALF, EARLY)
-        for bank, (first, last) in zip(u2[2:], gate_parts[2:]):
-            product(bank, first, w2_mx, first, last)
-        product(u1[2], EARLY, w1_mx, EARLY, 768)
-        product(u1[2], EARLY, w1_mx, 768, S)
+        for banks, weight in ((u2, w2_mx), (u1, w1_mx)):
+            product(banks[0], 0, weight, 0, FIRST)
+            product(banks[1], FIRST, weight, FIRST, WORDS_A)
+            product(banks[1], FIRST, weight, WORDS_A, EARLY)
+        for banks, weight in ((u2, w2_mx), (u1, w1_mx)):
+            product(banks[2], EARLY, weight, EARLY, WORDS_B)
+            product(banks[2], EARLY, weight, WORDS_B, S)
 
-        def looked_up(first, last):
+        def columns(first, last):
             return memory[:].indirect(slot_sb[:, entries(first, last)])
 
         gate = keep.tile([P, S], F32, name="gate")
@@ -150,15 +148,14 @@ def tile_picked_gmem_relu_p_kernel(tc, x_words, x_scales, mem, w1, w2, offs, slo
         new = reuse.tile([P, FIRST], F32, name="new", offset=0)
         old = keep.tile([P, S - FIRST], F32, name="old")
         nc.vector.scalar_tensor_tensor(taken[:], u1[0][:], 0.0, gate[:, :FIRST], ALU.max, ALU.mult)
-        nc.vector.tensor_tensor(kept[:], looked_up(0, FIRST), rest[:], ALU.mult)
-        nc.vector.tensor_copy(old[:, : SPLIT - FIRST], looked_up(FIRST, SPLIT))
-        nc.scalar.activation(old[:, SPLIT - FIRST :], looked_up(SPLIT, S), ACT.Copy)
-        for part in range(2, len(gate_parts)):
-            make_gate(part)
+        nc.vector.tensor_tensor(kept[:], columns(0, FIRST), rest[:], ALU.mult)
+        nc.vector.tensor_copy(old[:, : SPLIT - FIRST], columns(FIRST, SPLIT))
+        nc.scalar.activation(old[:, SPLIT - FIRST :], columns(SPLIT, S), ACT.Copy)
+        make_gate(2)
         nc.vector.tensor_tensor(new[:], taken[:], kept[:], ALU.add)
-        nc.scalar.activation(looked_up(0, FIRST), new[:], ACT.Copy)
+        nc.scalar.activation(columns(0, FIRST), new[:], ACT.Copy)
 
-        away = reuse.tile([P, S - FIRST], F32, name="away", offset=4 * FIRST)
+        away = reuse.tile([P, S - FIRST], F32, name="away", offset=F32_BYTES * FIRST)
         step = keep.tile([P, S - FIRST], F32, name="step")
         for bank, (first, last) in zip(u1[1:], cand_parts[1:]):
             part = slice(first - FIRST, last - FIRST)
@@ -166,6 +163,6 @@ def tile_picked_gmem_relu_p_kernel(tc, x_words, x_scales, mem, w1, w2, offs, slo
         for first, last in cand_parts[1:]:
             part = slice(first - FIRST, last - FIRST)
             nc.vector.tensor_tensor(step[:, part], away[:, part], gate[:, first:last], ALU.mult)
-        nc.vector.tensor_tensor(looked_up(FIRST, S), step[:], old[:], ALU.add)
+        nc.vector.tensor_tensor(columns(FIRST, S), step[:], old[:], ALU.add)
 
         nc.sync.dma_start(out, memory[:])

from contextlib import ExitStack

import concourse.mybir as mybir

K, T, S, N, U = 512, 2048, 1024, 128, 2048
FLOPS = 2 * 2 * K * N * S

F32 = mybir.dt.float32
BF16 = mybir.dt.bfloat16
I32 = mybir.dt.int32
U32 = mybir.dt.uint32
U16 = mybir.dt.uint16
U8 = mybir.dt.uint8
FP8X4 = mybir.dt.float8_e4m3fn_x4
ACT = mybir.ActivationFunctionType
ALU = mybir.AluOpType

P = 128
PACK = 4
LIST_ROWS = 16
BLOCKS = 16
STACK = P - BLOCKS
QUADRANT = 32
F32_BYTES = 4

EARLY = 640
MEM_FIRST = 512
FIRST = 256
SPLIT = 448
WORDS_A, WORDS_B = 512, 768
SHARED = 128


def tile_picked_gmem_relu_p_kernel(tc, x_words, x_scales, mem, w1, w2, offs, slot, out):
    nc = tc.nc
    with ExitStack() as ctx:
        keep = ctx.enter_context(tc.tile_pool(name="keep", bufs=1))
        reuse = ctx.enter_context(tc.tile_pool(name="reuse", bufs=1))
        psum = ctx.enter_context(tc.psum_pool(name="psum", bufs=1))

        offs_sb = keep.tile([P, S // LIST_ROWS], U16, name="offs_sb")
        slot_sb = keep.tile([P, S // LIST_ROWS], U16, name="slot_sb")
        words = keep.tile([P, T], U32, name="words", align_bytes=64)
        scales = keep.tile([P, T], U8, name="scales", align_bytes=64)
        memory = keep.tile([P, U], F32, name="memory", align_bytes=64)
        w2_raw = keep.tile([P, PACK, N], F32, name="w2_raw", tag="after_w2", align_bytes=64)
        w1_raw = keep.tile([P, PACK, N], F32, name="w1_raw", tag="after_w1", align_bytes=64)
        stacked = [
            keep.tile([P, EARLY], U8, name="stacked_early", align_bytes=64),
            reuse.tile([P, S - EARLY], U8, name="stacked_late", offset=F32_BYTES * FIRST - SHARED, align_bytes=64),
        ]
        planes = [keep.tile([P, n], U8, name="plane%d" % h, align_bytes=64) for h, n in enumerate((EARLY, S - EARLY))]

        def entries(first, last):
            return slice(first // LIST_ROWS, last // LIST_ROWS)

        nc.vector.memset(scales[:STACK, :].bitcast(I32), 0)
        for plane in planes:
            nc.vector.memset(plane[:].bitcast(I32), 0)

        nc.scalar.dma_start(scales[STACK:, :].bitcast(I32), x_scales[0].bitcast(I32))
        nc.sync.dma_start(offs_sb[:], offs)
        nc.sync.dma_start(words[:].bitcast(I32), x_words[0].rearrange("p n t -> p (n t)").bitcast(I32))
        nc.sync.dma_start(w2_raw[:], w2.rearrange("(p j) n -> p j n", j=PACK))
        nc.sync.dma_start(w1_raw[:], w1.rearrange("(p j) n -> p j n", j=PACK))
        nc.sync.dma_start(memory[:, :MEM_FIRST], mem[:, :MEM_FIRST])

        warm = keep.tile([P, 1], F32, name="warm")
        zero = keep.tile([P, 1], F32, name="zero")
        nc.vector.memset(zero[:], 0.0)
        nc.scalar.activation(warm[:], zero[:], ACT.Sigmoid)

        def pick_scales(part, first, last, queues):
            nc.vector.tensor_copy(stacked[part][:], scales[:].indirect(offs_sb[:, entries(first, last)]))
            for q, queue in zip((0, 2, 1, 3), queues):
                queue.dma_start(
                    planes[part][QUADRANT * q : QUADRANT * q + 4, :].bitcast(I32),
                    stacked[part][STACK + 4 * q : STACK + 4 * q + 4, :].bitcast(I32),
                )

        pick_scales(0, 0, EARLY, (nc.sync, nc.scalar, nc.sync, nc.scalar))
        nc.sync.dma_start(memory[:, MEM_FIRST:], mem[:, MEM_FIRST:])
        nc.sync.dma_start(slot_sb[:], slot)
        pick_scales(1, EARLY, S, (nc.gpsimd, nc.sync, nc.sync, nc.sync))

        def quantise(raw, name):
            grouped = keep.tile([P, N, PACK], BF16, name=name + "_grouped", align_bytes=64)
            nc.scalar.copy(grouped[:].rearrange("p (c i) j -> p c j i", i=4), raw[:].rearrange("p j (c i) -> p c j i", i=4))
            codes = keep.tile([P, N], U32, name=name + "_codes", align_bytes=64)
            plane = keep.tile([P, N], U8, name=name + "_scales", align_bytes=64)
            nc.vector.quantize_mx(out=codes[:].bitcast(FP8X4), scales=plane[:], in_=grouped[:].rearrange("p n j -> p (n j)"))
            return codes, plane

        picked = []

        def pick_words(first, last, **place):
            tile = keep.tile([P, last - first], U32, name="picked%d" % first, align_bytes=64, **place)
            nc.vector.tensor_copy(tile[:], words[:].indirect(offs_sb[:, entries(first, last)]))
            picked.append((tile, first))

        pick_words(0, WORDS_A)
        w2_mx = quantise(w2_raw, "w2")
        pick_words(WORDS_A, WORDS_B, tag="after_w2")
        w1_mx = quantise(w1_raw, "w1")
        pick_words(WORDS_B, S, tag="after_w1")

        def product(bank, base, weight, first, last):
            tile, start = [(t, a) for t, a in picked if a <= first][-1]
            part, origin = (0, 0) if first < EARLY else (1, EARLY)
            nc.tensor.matmul_mx(
                out=bank[:, first - base : last - base],
                lhsT=weight[0][:].bitcast(FP8X4),
                lhsT_scale=weight[1][:],
                rhs=tile[:, first - start : last - start].bitcast(FP8X4),
                rhs_scale=planes[part][:, first - origin : last - origin],
                start=True,
                stop=True,
            )

        gate_parts = [(0, FIRST), (FIRST, EARLY), (EARLY, S)]
        cand_parts = [(0, FIRST), (FIRST, EARLY), (EARLY, S)]
        u2 = [psum.tile([P, b - a], F32, name="u2_%d" % a) for a, b in gate_parts]
        u1 = [psum.tile([P, b - a], F32, name="u1_%d" % a) for a, b in cand_parts]
        for banks, weight in ((u2, w2_mx), (u1, w1_mx)):
            product(banks[0], 0, weight, 0, FIRST)
            product(banks[1], FIRST, weight, FIRST, WORDS_A)
            product(banks[1], FIRST, weight, WORDS_A, EARLY)
        for banks, weight in ((u2, w2_mx), (u1, w1_mx)):
            product(banks[2], EARLY, weight, EARLY, WORDS_B)
            product(banks[2], EARLY, weight, WORDS_B, S)

        def columns(first, last):
            return memory[:].indirect(slot_sb[:, entries(first, last)])

        gate = keep.tile([P, S], F32, name="gate")
        rest = keep.tile([P, FIRST], F32, name="rest")

        def make_gate(part):
            first, last = gate_parts[part]
            nc.scalar.activation(gate[:, first:last], u2[part][:], ACT.Sigmoid)

        make_gate(0)
        nc.scalar.activation(rest[:], u2[0][:], ACT.Sigmoid, scale=-1.0)
        make_gate(1)

        taken = keep.tile([P, FIRST], F32, name="taken")
        kept = keep.tile([P, FIRST], F32, name="kept")
        new = reuse.tile([P, FIRST], F32, name="new", offset=0)
        old = keep.tile([P, S - FIRST], F32, name="old")
        nc.vector.scalar_tensor_tensor(taken[:], u1[0][:], 0.0, gate[:, :FIRST], ALU.max, ALU.mult)
        nc.vector.tensor_tensor(kept[:], columns(0, FIRST), rest[:], ALU.mult)
        nc.vector.tensor_copy(old[:, : SPLIT - FIRST], columns(FIRST, SPLIT))
        nc.scalar.activation(old[:, SPLIT - FIRST :], columns(SPLIT, S), ACT.Copy)
        make_gate(2)
        nc.vector.tensor_tensor(new[:], taken[:], kept[:], ALU.add)
        nc.scalar.activation(columns(0, FIRST), new[:], ACT.Copy)

        away = reuse.tile([P, S - FIRST], F32, name="away", offset=F32_BYTES * FIRST)
        step = keep.tile([P, S - FIRST], F32, name="step")
        for bank, (first, last) in zip(u1[1:], cand_parts[1:]):
            part = slice(first - FIRST, last - FIRST)
            nc.vector.scalar_tensor_tensor(away[:, part], bank[:], 0.0, old[:, part], ALU.max, ALU.subtract)
        for first, last in cand_parts[1:]:
            part = slice(first - FIRST, last - FIRST)
            nc.vector.tensor_tensor(step[:, part], away[:, part], gate[:, first:last], ALU.mult)
        nc.vector.tensor_tensor(columns(FIRST, S), step[:], old[:], ALU.add)

        nc.sync.dma_start(out, memory[:])
